import numpy as np, ml_dtypes
CORES = [51,54,179,182]
N = 4
BF = ml_dtypes.bfloat16
def gentries(a):
    return np.ascontiguousarray(a.reshape(8, 16, -1).transpose(0, 2, 1)).reshape(8, -1)
def gtable(e):
    e = np.asarray(e); return np.ascontiguousarray(e.reshape(8, -1, 16).transpose(0, 2, 1)).reshape(128, -1).astype(np.int32)
NV, YM, P, LG, S, B, D0, D1 = 2048, 512, 1024, 4, 3, 2, 800, 1000
def lst(a):
    return np.stack([gentries(b) for b in a]).astype(np.int64)
def walk(V, st, x, y, dx, dy, E, kp=None, L=None):
    logs = []
    for j in range(LG):
        for s in range(S):
            v = 64 * (y >> 4) + (x >> 4); e = E >> 6; d = np.zeros_like(E)
            for h in range(N):
                q = (h + j) % N
                a = np.take_along_axis(V[q], v[h][:, None, :], 2)
                d[h] = np.add.reduce(a * np.take_along_axis(st[q], e[h][:, None, :], 2), axis=1)
                if L is not None: L[h] += a * np.take_along_axis(kp[q], e[h][:, None, :], 2)
            E = np.maximum(E - d, 0)
            if j < LG - 1 or s < S - 1:
                t = np.where(d >= D1, 1, np.where(d >= D0, 2, 4))
                x = (x + t * dx) & 1023; y = (y + t * dy) & (YM - 1)
        logs.append(v)
    return E, logs
def verdict(E, F):
    s = np.sign(E - F)
    return np.sign(2 * s + np.add.reduce(s, axis=1, keepdims=True))
def mend(V, cor, logs, t):
    for q in range(N):
        for j in range(LG):
            h = (q - j) % N
            w = np.take_along_axis(cor[q], logs[j][h] // P * P + np.arange(P), 1)[:, None, :]
            a = np.take_along_axis(V[q], w, 2)
            np.put_along_axis(V[q], w, np.where(a > 0, np.minimum(a + t[h][:, None, :], 15), 0).astype(V.dtype), 2)
def parts(rng):
    a = {"V": rng.integers(0, 16, (N, 8, 16, NV)).astype(np.int32), "st": rng.integers(0, 16, (N, 8, 16, 1024)).astype(np.int32), "kp": np.exp2(5 * rng.random((N, 8, 16, 1024)) - 3)}
    for k, hi in (("x", 1024), ("y", YM), ("dx", 1024), ("dy", YM), ("E", 65536)): a[k] = rng.integers(0, hi, (N, 8, B, P))
    a["cor"] = np.ascontiguousarray(np.argsort(rng.random((N, 8, NV)), axis=-1))
    return a
def signs(rng):
    lean = rng.random((B - 1, N, 1, P))
    return np.where(rng.random((B - 1, N, 8, P)) < 0.25, 0, np.where(rng.random((B - 1, N, 8, P)) < lean, 1, -1))
def finish(rng, a, s=None, F=None, one=False, calm=False):
    V = a["V"].copy(); ev = (np.arange(8) % 2 == 0)[None, :, None]; out = []
    if s is None: s = signs(rng)
    for b in range(B if calm else B - 1):
        x, y, dx, dy = [a[k][:, :, b] for k in ("x", "y", "dx", "dy")]; E0 = a["E"][:, :, b]
        if calm:
            w = walk(V, a["st"], x, y, dx, dy, np.where(ev, 63, E0))[0]
            E0 = np.where(ev, np.minimum(63 - w + rng.integers(0, 4, w.shape), 63), E0); a["E"][:, :, b] = E0
            if b == B - 1: break
        E, logs = walk(V, a["st"], x, y, dx, dy, E0)
        if F is None:
            big = np.where(rng.random(E.shape) < 0.4, 1, rng.integers(1, 2000, E.shape))
            m = np.clip(E - s[b] * (1 if one else big), 0, 65535)
            if calm: m = np.where(ev, rng.integers(0, 4, E.shape), m)
        else: m = F[:, :, b]
        out.append(m); mend(V, a["cor"], logs, verdict(E, m))
    g = lambda z: np.stack([gtable(c.reshape(8, -1)) for c in z])
    r = {"slab": a["V"].reshape(N, 128, NV).astype(np.float32).astype(BF), "spow": a["st"].reshape(N, 128, 1024).astype(np.float32).astype(BF), "kap": a["kp"].reshape(N, 128, 1024).astype(np.float32).astype(BF)}
    for n, k in (("px", "x"), ("py", "y"), ("vx", "dx"), ("vy", "dy"), ("en", "E")): r[n] = g(a[k])
    r["fm"] = g(np.stack(out, axis=2)); r["cor"] = g(a["cor"])
    return r
def setup_inputs(rng):
    return finish(rng, parts(rng))
def setup_inputs_spread(rng):
    a = parts(rng); top = np.array([1, 2, 4, 8, 16, 16, 16])
    a["V"] = np.floor(rng.random((N, 8, 16, NV)) * rng.choice(top, (N, 8, 1, NV))).astype(np.int32)
    a["st"] = np.floor(rng.random((N, 8, 16, 1024)) * rng.choice(top, (N, 8, 1, 1024))).astype(np.int32)
    a["kp"] = np.exp2(rng.integers(-3, 2, (N, 8, 1, 1024))) * (1 + rng.random((N, 8, 16, 1024)))
    a["E"] = np.minimum(np.exp2(6 + 10 * rng.random((N, 8, B, P))).astype(np.int64), 65535)
    a["dx"] = np.exp2(9.99 * rng.random((N, 8, B, P))).astype(np.int64)
    return finish(rng, a)
def setup_inputs_ends(rng):
    a = parts(rng)
    def mixed(n):
        k = rng.integers(0, 4, (N, 8, 1, n))
        return np.where(k == 0, 15, np.where(k == 1, 0, 15 * rng.integers(0, 2, (N, 8, 16, n)))).astype(np.int32)
    a["V"] = mixed(NV); a["st"] = mixed(1024); a["kp"] = 4.0 * (rng.random((N, 8, 16, 1024)) < 0.4)
    for k, hi in (("x", 1023), ("y", YM - 1), ("dx", 1023), ("dy", YM - 1)): a[k] = hi * rng.integers(0, 2, (N, 8, B, P))
    a["E"] = 65535 * (rng.random((N, 8, B, P)) < 0.7).astype(np.int64)
    a["st"][:, 7] = np.where(rng.random((N, 1, 1024)) < 0.7, 15, a["st"][:, 7])
    a["st"][:, 7, :, 1023] = 15
    a["st"][:, 3, :, 1023] = 0
    for g in (3, 7):
        a["kp"][:, g, :, 1023] = 4.0
        for v in (0, 63, NV - 64, NV - 1): a["V"][:, g, :, v] = 15
        for p in (0, 1, P - 2, P - 1):
            a["x"][:, g, :, p] = 1023; a["y"][:, g, :, p] = YM - 1; a["dx"][:, g, :, p] = 0; a["dy"][:, g, :, p] = 0; a["E"][:, g, :, p] = 65535
    z = np.zeros(NV, np.int64); z[0::2] = np.arange(NV // 2); z[1::2] = NV - 1 - np.arange(NV // 2)
    for q in range(N):
        for g in range(8): a["cor"][q, g] = np.roll(z, int(rng.integers(0, NV)))
    return finish(rng, a, F=65535 * rng.integers(0, 2, (N, 8, B - 1, P)))
def setup_inputs_corners(rng):
    a = parts(rng); kd = (rng.permutation(8)[None, :] + np.arange(N)[:, None]) % 8
    first = P * np.arange(NV // P); edge = np.concatenate([first, first + P - 1])
    for q in range(N):
        for g in range(8):
            c = int(kd[q, g])
            if c in (0, 1, 2): a["V"][q, g] = (0, 15, 1)[c]
            if c in (3, 4): a["V"][q, g] = rng.integers(0, 2, (16, NV)) + (0 if c == 3 else 14)
            if c in (0, 1):
                a["x"][q, g] = 1023 * c; a["y"][q, g] = (YM - 1) * c; a["dx"][q, g] = 0; a["dy"][q, g] = 0
            if c == 2:
                a["x"][q, g] = 1023 - rng.integers(0, 2, (B, P)); a["y"][q, g] = YM - 1 - rng.integers(0, 2, (B, P)); a["dx"][q, g] = 1; a["dy"][q, g] = 1
            if c == 3:
                v = rng.choice(edge, (B, P))
                a["x"][q, g] = 16 * (v & 63) + rng.integers(0, 16, (B, P)); a["y"][q, g] = 16 * (v >> 6) + rng.integers(0, 16, (B, P)); a["dx"][q, g] = 0; a["dy"][q, g] = 0
            if c == 4: a["dx"][q, g] = 1023; a["dy"][q, g] = YM - 1
            if c == 5: a["E"][q, g] = rng.choice(np.array([0, 1, 63, 64, 65535]), (B, P))
            if c == 6: a["E"][q, g] = rng.integers(0, 3601, (B, P))
            if c == 1: a["cor"][q, g] = np.arange(NV)
            if c == 2: a["cor"][q, g] = np.arange(NV)[::-1]
    t = np.array([[1] * 8, [-1] * 8, [1] * 7 + [0], [-1] * 7 + [0], [1] * 7 + [-1], [-1] * 7 + [1], [1, -1] * 4, [1] + [0] * 7, [-1] + [0] * 7, [0] * 8,
                  [1, -1, -1, -1, 0, 0, 0, 0], [1, -1, -1, -1, -1, 0, 0, 0], [-1, 1, 1, 1, 0, 0, 0, 0], [-1, 1, 1, 1, 1, 0, 0, 0]])
    i = rng.integers(0, 14, (B - 1, N, 1, P)); o = rng.integers(0, 8, (B - 1, N, 1, P))
    return finish(rng, a, s=t[i, (np.arange(8)[None, None, :, None] + o) % 8])
def setup_inputs_ties(rng):
    a = parts(rng); t = rng.choice(np.array([D0 - 1, D0, D1 - 1, D1]), (N, 8, 1024)); t[..., D0 >> 6] = D0
    m = t // 15; k = np.argsort(rng.random((N, 8, 15, 1024)), axis=2)
    st = np.concatenate([(m // 15)[:, :, None] + (k < (m % 15)[:, :, None]), (t - 15 * m)[:, :, None]], axis=2)
    u = np.array([15] * 15 + [1]); pm = np.argsort(rng.random((N, 8, 16)), axis=-1)
    st = np.take_along_axis(st, pm[..., None], 2); v = np.broadcast_to(u[pm][..., None], (N, 8, 16, NV))
    a["V"][:, ::2] = v[:, ::2]; a["st"][:, ::2] = st[:, ::2]
    p = np.arange(P) % 4; E = a["E"]
    E = np.where(p == 0, D0 + rng.integers(-1, 2, E.shape), np.where(p == 1, 64 * rng.integers(1, 1024, E.shape) - rng.integers(0, 2, E.shape), E))
    a["E"][:, ::2] = E[:, ::2]
    return finish(rng, a, one=True)
def setup_inputs_calm(rng):
    a = parts(rng)
    v = np.where(rng.random((N, 8, 16, NV)) < 0.25, rng.integers(1, 4, (N, 8, 16, NV)), 0); a["V"][:, ::2] = v[:, ::2]
    k = np.argsort(rng.random((N, 8, 16)), axis=-1) < 2
    a["st"][:, ::2, :, 0] = k[:, ::2]
    return finish(rng, a, calm=True)
def check_ranges(d):
    bad = []
    for k, lo, hi in (("slab", 0, 15), ("spow", 0, 15), ("kap", 0, 4), ("px", 0, 1023), ("py", 0, YM - 1), ("vx", 0, 1023), ("vy", 0, YM - 1), ("en", 0, 65535), ("fm", 0, 65535), ("cor", 0, NV - 1)):
        a = np.asarray(d[k]).astype(np.float64)
        if not (np.min(a) >= lo and np.max(a) <= hi): bad.append("range of " + k)
        elif k in ("slab", "spow") and np.any(a != np.floor(a)): bad.append("whole numbers of " + k)
    if np.any(np.sort(lst(np.asarray(d["cor"])), axis=-1) != np.arange(NV)): bad.append("each voxel once in cor")
    return bad
def reference(slab, spow, kap, px, py, vx, vy, en, fm, cor):
    V = slab.astype(np.float32).astype(np.int32).reshape(N, 8, 16, NV); st = spow.astype(np.float32).astype(np.int32).reshape(N, 8, 16, 1024)
    kp = kap.astype(np.float64).reshape(N, 8, 16, 1024); x, y, dx, dy, E0 = [lst(a).reshape(N, 8, B, P) for a in (px, py, vx, vy, en)]
    F = lst(fm).reshape(N, 8, B - 1, P); cl = lst(cor); L = np.zeros((N, 8, 16, P)); E = np.zeros((N, 8, B, P), np.int64)
    for b in range(B):
        E[:, :, b], logs = walk(V, st, x[:, :, b], y[:, :, b], dx[:, :, b], dy[:, :, b], E0[:, :, b], kp, L)
        if b < B - 1: mend(V, cl, logs, verdict(E[:, :, b], F[:, :, b]))
    ye = np.stack([gtable((E[r] & 1023).reshape(8, B * P)) for r in range(N)])
    return {"yl": np.exp(L * -0.0078125).reshape(N, 128, P).astype(np.float32), "ye": ye.astype(np.float32)}

def check_inputs(d):
    bad = list(check_ranges(d))
    if not bad:
        for name, y in reference(**d).items():
            for q in range(N):
                v = np.abs(np.asarray(y[q], np.float64))
                if v.max() > 5 * np.sqrt(np.mean(v * v)): bad.append('%s of rank %d is uneven' % (name, q))
    return bad

@@ -1,0 +1,488 @@
+from concourse.bass import DstId, RemoteDMATransfer
+from concourse.mybir import AluOpType as Op, ActivationFunctionType as Fn
+
+N, NV, NE, P, S, B = 4, 2048, 1024, 1024, 3, 2
+NS = N * S
+CH = 256
+YS = 13
+IOFF = 32
+IOT0 = 32
+BY_SCALAR = [0] + [6] * 10 + [8] * 12 + [0]
+FIRST = [2] + [3] * 9 + [1] + [3] * 13
+SCATTER = [20] + [12] * 9 + [0] * 2
+REORDER = [0] * 10 + [32, 96]
+
+SCRATCH = {
+    "PX": ("sbuf", [128, 128], "int32"), "PY": ("sbuf", [128, 128], "int32"), "VX": ("sbuf", [128, 128], "int32"),
+    "VY": ("sbuf", [128, 128], "int32"), "EN": ("sbuf", [128, 128], "int32"), "FM": ("sbuf", [128, 64], "int32"),
+    "COR": ("sbuf", [128, 128], "int32"),
+    "IOI": ("sbuf", [128, 144], "int32"), "PCI": ("sbuf", [128, 4], "int32"), "PCF": ("sbuf", [128, 4], "float32"),
+    "W": ("sbuf", [128, 144], "bfloat16"), "IDB": ("sbuf", [128, 128], "bfloat16"), "IDF": ("sbuf", [128, 128], "float32"),
+    "ZB": ("sbuf", [128, 512], "bfloat16"), "BD": ("sbuf", [128, 128], "bfloat16"), "SEL": ("sbuf", [128, 16], "float32"),
+    "M2": ("sbuf", [128, 128], "bfloat16"), "BR": ("sbuf", [128, 2048], "bfloat16"),
+    "I1": ("sbuf", [128, 128], "int32"), "I2": ("sbuf", [128, 128], "int32"), "I3": ("sbuf", [128, 128], "int32"),
+    "F1": ("sbuf", [128, 128], "float32"), "F2": ("sbuf", [128, 128], "float32"), "H1": ("sbuf", [128, 128], "bfloat16"),
+    "D2": ("sbuf", [128, 128], "float32"),
+    "Z": ("sbuf", [128, 64], "int32"), "ZW": ("sbuf", [128, 64], "int32"), "Q": ("sbuf", [128, 64], "int32"),
+    "MD": ("sbuf", [128, 64], "float32"), "XH": ("sbuf", [128, 64], "int32"),
+    "YH": ("sbuf", [128, 64], "int32"), "V": ("sbuf", [128, 64], "int32"), "U": ("sbuf", [128, 128], "float32"),
+    "VI": ("sbuf", [128, 128], "uint16"), "EI": ("sbuf", [128, 128], "uint16"),
+    "A": ("sbuf", [128, 2048], "bfloat16"), "K": ("sbuf", [128, 2048], "bfloat16"), "PR": ("sbuf", [128, 1024], "bfloat16"),
+    "AK": ("sbuf", [128, 2048], "float32"),
+    "CU": ("sbuf", [128, 128], "uint16"), "PU": ("sbuf", [128, 128], "uint16"), "IOT": ("sbuf", [128, 2048], "float32"),
+    "INVW": ("sbuf", [128, 2048], "float32"), "INVL": ("sbuf", [128, 128], "float32"), "INVU": ("sbuf", [128, 128], "uint16"),
+    "AC": ("sbuf", [128, 2048], "bfloat16"), "CS": ("sbuf", [128, 2048], "bfloat16"), "QQ": ("sbuf", [128, 1024], "bfloat16"),
+    "R": ("sbuf", [128, 2048], "bfloat16"),
+    "KM": ("sbuf", [128, 512], "bfloat16"), "TY": ("sbuf", [128, 512], "bfloat16"), "TO": ("sbuf", [128, 512], "bfloat16"),
+    "TL": ("sbuf", [128, 512], "bfloat16"), "UF": ("sbuf", [128, 64], "float32"), "NF": ("sbuf", [128, 64], "float32"),
+    "Z2": ("sbuf", [128, 64], "float32"), "SG": ("sbuf", [128, 64], "bfloat16"),
+    "MN": ("sbuf", [128, 512], "bfloat16"), "HM": ("sbuf", [128, 512], "bfloat16"), "SS": ("sbuf", [128, 128], "bfloat16"),
+    "E1": ("sbuf", [128, 64], "int32"), "E2": ("sbuf", [128, 64], "int32"), "YE": ("sbuf", [128, 128], "float32"),
+    "YL": ("sbuf", [128, 1024], "float32"),
+}
+for _q in range(N):
+    SCRATCH["TAB%d" % _q] = ("sbuf", [128, NV + 2 * NE], "bfloat16")
+    SCRATCH["SL%d" % _q] = ("sbuf", [128, NV], "bfloat16")
+for _b in range(8):
+    SCRATCH["PS%d" % _b] = ("psum", [128, 512], "float32")
+SEMAPHORES = (["cv", "cs", "cp", "cg", "sent", "tm"] + [_p + str(_q) for _q in range(N) for _p in ("slab", "spow", "kap", "sl")]
+              + ["d%d" % _i for _i in range(14)])
+
+LB, AB, PA, PB = (0, 1), (2, 3, 4, 5), 6, 7
+
+
+def bits(engines):
+    m = 0
+    for e in engines:
+        m |= 1 << e
+    return m
+
+
+def rank_program(g, core, T, topo):
+    rank = T.rank_of(core)
+    if rank is None:
+        return
+    cores = T.cores
+    eng = {"v": g.vector, "s": g.scalar, "p": g.tensor, "g": g, "y": g.sync}
+    count = {}
+    known = {q: {} for q in eng}
+    wrote, read, bank = {}, {}, {}
+    ndma = [0]
+
+    def wait(q, ev):
+        sem, val, clock, _ = ev
+        if known[q].get(sem, 0) >= val:
+            return
+        eng[q].wait_ge(T.sem[sem], val)
+        for k, x in list(clock.items()) + [(sem, val)]:
+            if known[q].get(k, 0) < x:
+                known[q][k] = x
+
+    def op(q, fn, r=(), w=(), b=(), dma=False, remote=0):
+        need = [wrote[t] for t in r if t in wrote] + [wrote[t] for t in w if t in wrote]
+        for t in w:
+            need += read.get(t, [])
+        for k in b:
+            need += [e for qq, e in bank.get(k, {}).items() if qq != q]
+        best = {}
+        for e in need:
+            if q == "p" and e[3] == "p":
+                continue
+            if e[0] not in best or best[e[0]][1] < e[1]:
+                best[e[0]] = e
+        for e in sorted(best.values(), key=lambda e: -len(e[2])):
+            wait(q, e)
+        ins = fn()
+        if remote:
+            sem, inc = "sent", remote
+        elif dma:
+            sem, inc = "d%d" % ndma[0], 16
+            ndma[0] += 1
+            ins.then_inc(T.sem[sem], 16)
+        else:
+            sem, inc = "c" + q, 1
+            ins.then_inc(T.sem[sem], 1)
+        count[sem] = count.get(sem, 0) + inc
+        ev = (sem, count[sem], dict(known[q]), q)
+        if not remote:
+            for t in r:
+                read.setdefault(t, []).append(ev)
+        for t in w:
+            wrote[t] = ev
+            read[t] = []
+        for k in b:
+            bank.setdefault(k, {})[q] = ev
+
+    def arrives(token, sem, val):
+        count[sem] = val
+        wrote[token] = (sem, val, {}, "x")
+
+    def ts(out, in0, s1, o0, s2=None, o1=None, r=(), w=(), b=()):
+        if o1 is None:
+            op("v", lambda: g.vector.tensor_scalar(out, in0, s1, None, o0), r, w, b)
+        else:
+            op("v", lambda: g.vector.tensor_scalar(out, in0, s1, s2, o0, o1), r, w, b)
+
+    def tt(out, in0, in1, o, r=(), w=(), b=()):
+        op("v", lambda: g.vector.tensor_tensor(out, in0, in1, o), r, w, b)
+
+    def cp(out, in_, r=(), w=(), b=()):
+        op("v", lambda: g.vector.tensor_copy(out, in_), r, w, b)
+
+    def act(out, in_, f, r=(), w=(), b=(), **kw):
+        op("s", lambda: g.scalar.activation(out, in_, f, **kw), r, w, b)
+
+    def mm(seq, r=(), b=()):
+        def run():
+            ins = None
+            for out, lhsT, rhs, start, stop in seq:
+                ins = g.tensor.matmul(out, lhsT, rhs, start, stop)
+            return ins
+        op("p", run, r, (), b)
+
+    PS = [T["PS%d" % k] for k in range(8)]
+
+    def near(a, b):
+        return cores[b] in topo.cores_of(cores[a])
+
+    def lanes(a):
+        far = [d for d in range(N) if not near(a, d)]
+        mate = [d for d in range(N) if d != a and near(a, d)]
+        off = topo.engines(cores[a], cores[far[0]])
+        on = [e for e in topo.engines(cores[a], cores[mate[0]]) if e not in off]
+        return off, on
+
+    def source_of(q, d):
+        if near(q, d):
+            return q
+        first = min((x for x in range(N) if near(x, d)), key=lambda x: (q - x) % N)
+        return q if first == d else first
+
+    def lane(a, d):
+        return lanes(a)[1 if near(a, d) else 0]
+
+    def send(dests, src, dst, sem, r):
+        trs, tot = [], 0
+        for d in dests:
+            rid, pid = topo.addr(cores[d], core)
+            trs.append(RemoteDMATransfer(dst_ids=[DstId(rid=rid, pnc=pid)], dma_engine_mask=bits(lane(rank, d)),
+                                         remote_sem=T.sem[sem], src=src, dst=dst))
+            tot += len(lane(rank, d))
+        op("g", lambda: g.remote_dma_fused(trs, local_sem=T.sem.sent), r, (), remote=tot)
+
+    def verdict_lane(a, d):
+        off, on = lanes(a)
+        far = [x for x in range(N) if not near(a, x)]
+        h = len(off) // len(far)
+        return on[:h] if near(a, d) else off[far.index(d) * h:(far.index(d) + 1) * h]
+
+    direct = [d for d in range(N) if d != rank and source_of(rank, d) == rank]
+    passes = [(q, d) for j in range(1, N) for q in [(rank + j) % N] for d in range(N)
+              if d not in (rank, q) and source_of(q, d) == rank]
+    for q in range(N):
+        if q != rank:
+            a = source_of(q, rank)
+            n = len(lane(a, rank))
+            for part in ("slab", "spow", "kap"):
+                arrives((part, q), (part if a == q else "slab") + str(q), n)
+            arrives(("sl", q, 0), "sl%d" % q, n)
+            arrives(("sl", q, 1), "sl%d" % q, n)
+    arrives("TL", "tm", sum(len(verdict_lane(a, rank)) for a in range(N) if a != rank))
+
+    TAB = T["TAB%d" % rank]
+
+    def load(q, out, in_, w):
+        op(q, lambda: eng[q].dma_start(out, in_), (), [w], dma=True)
+
+    load("y", T.PX[:], T.px[:], "PX")
+    load("s", T.PY[:], T.py[:], "PY")
+    load("y", T.COR[:], T.cor[:], "COR")
+    load("s", T.EN[:], T.en[:], "EN")
+    load("y", TAB[:, 0:NV], T.slab[:], ("slab", rank))
+    load("s", T.VY[:], T.vy[:], "VY")
+    load("s", T.VX[:], T.vx[:], "VX")
+    load("y", TAB[:, NV:NV + NE], T.spow[:], ("spow", rank))
+    load("y", TAB[:, NV + NE:], T.kap[:], ("kap", rank))
+    load("y", T.FM[:], T.fm[:], "FM")
+
+    def positions(i, c0, c1):
+        op("g", lambda: g.iota(T.IOT[:, 16 * c0:16 * c1], [[1, c1 - c0], [128, 16]], IOFF + c0, 0,
+                               allow_small_or_imprecise_dtypes=True), (), [("IOT", i)])
+
+    op("g", lambda: g.iota(T.PCI[:], [[0, 4]], 0, 1), (), ["PCI"])
+    op("g", lambda: g.iota(T.IOI[:], [[1, 144]], 0, 0), (), ["IOI"])
+    positions(0, 0, IOT0)
+    for part, c0, c1 in (("slab", 0, NV), ("spow", NV, NV + NE), ("kap", NV + NE, NV + 2 * NE)):
+        send(direct, TAB[:, c0:c1], TAB[:, c0:c1], part + str(rank), [(part, rank)])
+    positions(1, IOT0, 128)
+    for q, d in passes:
+        send([d], T["TAB%d" % q][:], T["TAB%d" % q][:], "slab%d" % q, [("slab", q), ("spow", q), ("kap", q)])
+
+    op("v", lambda: g.vector.memset(T.ZB[:], 0.0), (), ["ZB"])
+    ts(T.PCI[:, 1:2], T.PCI[:, 0:1], 112, Op.bitwise_and, r=["PCI"], w=["PC1"])
+    ts(T.PCI[:, 2:3], T.PCI[:, 0:1], 15, Op.bitwise_and, r=["PCI"], w=["PC2"])
+    cp(T.PCF[:], T.PCI[:], ["PCI", "PC1", "PC2"], ["PCF"])
+    pk, pg, pr = T.PCF[:, 0:1], T.PCF[:, 1:2], T.PCF[:, 2:3]
+    ts(T.I1[:], T.IOI[:, 0:128], 112, Op.bitwise_and, r=["IOI"], w=["I1"])
+    ts(T.SEL[:], T.IOI[:, 0:16], pr, Op.is_equal, r=["IOI", "PCF"], w=["SEL"])
+    ts(T.BD[:], T.I1[:], pg, Op.is_equal, r=["I1", "PCF"], w=["BD"])
+    ts(T.W[:], T.IOI[:], 15.0, Op.subtract, pg, Op.is_equal, r=["IOI", "PCF"], w=["W"])
+    ts(T.IDB[:], T.IOI[:, 0:128], pk, Op.is_equal, r=["IOI", "PCF"], w=["IDB"])
+    ts(T.IDF[:], T.IOI[:, 0:128], pk, Op.is_equal, r=["IOI", "PCF"], w=["IDF"])
+    ts(T.I2[:], T.IOI[:, 0:128], 15, Op.bitwise_and, r=["IOI"], w=["I2"])
+    ts(T.F1[:], T.IDF[:], 2.0, Op.mult, r=["IDF"], w=["F1"])
+    ts(T.H1[:], T.I2[:], pr, Op.is_equal, r=["I2", "PCF"], w=["H1"])
+    tt(T.M2[:], T.H1[:], T.F1[:], Op.add, ["H1", "F1"], ["M2"])
+    for k in LB:
+        mm([(PS[k][:], T.ZB[:, 0:128], T.ZB[:], True, False)], ["ZB"], [k])
+    for k in range(16):
+        act(T.BR[:, 128 * k:128 * k + 128], T.BD[:], Fn.Copy, ["BD", "SEL"], [("BR", k)], scale=T.SEL[:, k:k + 1])
+
+    def voxel(par):
+        ts(T.XH[:], T.Z[:], 4, Op.arith_shift_right, 63, Op.bitwise_and, r=["Z"], w=["XH"])
+        ts(T.YH[:], T.Z[:], YS - 2, Op.arith_shift_right, 31 << 6, Op.bitwise_and, r=["Z"], w=["YH"])
+        tt(T.V[:], T.XH[:], T.YH[:], Op.add, ["XH", "YH"], ["V"])
+        cp(T.VI[:, 64 * par:64 * par + 64], T.V[:], ["V"], [("VI", par)])
+
+    def record(par, src, tok):
+        ts(T.EI[:, 64 * par:64 * par + 64], src, 1.0 / 64, Op.mult, -31.5 / 64, Op.add, r=[tok], w=[("EI", par)])
+
+    def wrap():
+        ts(T.ZW[:], T.Z[:], (511 << YS) | 1023, Op.bitwise_and, r=["Z"], w=["ZW"])
+
+    def begin(b):
+        c = slice(64 * b, 64 * b + 64)
+        ts(T.MD[:], T.PY[:, c], float(1 << YS), Op.mult, r=["PY"], w=["MD"])
+        tt(T.Z[:], T.MD[:], T.PX[:, c], Op.add, ["MD", "PX"], ["Z"])
+        voxel(0)
+        record(0, T.EN[:, c], "EN")
+        wrap()
+
+    begin(0)
+    ts(T.I1[:], T.COR[:], 15, Op.bitwise_and, r=["COR"], w=["I1"])
+    ts(T.I3[:], T.COR[:], 4, Op.arith_shift_right, r=["COR"], w=["I3"])
+    ts(T.F1[:], T.I1[:], 128.0, Op.mult, r=["I1"], w=["F1"])
+    cp(T.CU[:], T.COR[:], ["COR"], ["CU"])
+    tt(T.I2[:], T.F1[:], T.I3[:], Op.add, ["F1", "I3"], ["I2"])
+    cp(T.PU[:], T.I2[:], ["I2"], ["PU"])
+    ts(T.I1[:], T.VY[:], 256.0, Op.add, r=["VY"], w=["I1"])
+    ts(T.F2[:], T.VX[:], 2.0, Op.mult, r=["VX"], w=["F2"])
+    ts(T.I2[:], T.I1[:], 511, Op.bitwise_and, r=["I1"], w=["I2"])
+    ts(T.F1[:], T.I2[:], -256.0, Op.add, float(2 << YS), Op.mult, r=["I2"], w=["F1"])
+    tt(T.D2[:], T.F1[:], T.F2[:], Op.add, ["F1", "F2"], ["D2"])
+
+    def table(t):
+        return (rank + (t % NS) // S) % N
+
+    def lmul(t, u0, u1):
+        par, q, nx = t % 2, table(t), BY_SCALAR[t]
+        o = 1024 * par
+        u = u0
+        while u < u1:
+            if u < nx:
+                e = min(u1, nx, u // 4 * 4 + 4)
+                k = AB[2 * par + u // 4]
+                tt(T.AK[:, o + 128 * u:o + 128 * e], PS[k][:, 128 * (u % 4):128 * (u % 4 + e - u)], T.K[:, o + 128 * u:o + 128 * e],
+                   Op.mult, [("K", par)], [("AK", par, i) for i in range(u, e)], [k])
+            else:
+                e = u1
+                win = T["TAB%d" % q][:, NV + NE:].indirect(T.EI[:, 64 * par + 8 * u:64 * par + 8 * e])
+                tt(T.AK[:, o + 128 * u:o + 128 * e], win, T.A[:, o + 128 * u:o + 128 * e], Op.mult,
+                   [("kap", q), ("EI", par)] + [("A", par, i // 2) for i in range(u, e)], [("AK", par, i) for i in range(u, e)])
+            u = e
+
+    def lacc(t, u0, u1, last=False):
+        o = 1024 * (t % 2)
+        u = u0
+        while u < u1:
+            e = min(u1, u // 4 * 4 + 4)
+            mm([(PS[LB[u // 4]][:, 128 * (u % 4):128 * (u % 4 + e - u)], T.IDF[:], T.AK[:, o + 128 * u:o + 128 * e], False,
+                 last and e % 4 == 0)], ["IDF"] + [("AK", t % 2, i) for i in range(u, e)], [LB[u // 4]])
+            u = e
+
+    def acopy(t, h):
+        par, n = t % 2, 128 * min(4, BY_SCALAR[t] - 4 * h)
+        if n > 0:
+            k, o = AB[2 * par + h], 1024 * par + 512 * h
+            mm([(PS[k][:, 0:n], T.IDB[:], T.A[:, o:o + n], True, True)], ["IDB", ("A", par, 2 * h), ("A", par, 2 * h + 1)], [k])
+
+    def energies(b, src, tok):
+        ts(T.E1[:], src, 0.0, Op.max, r=[tok], w=["E1"])
+        ts(T.E2[:], T.E1[:], 1023, Op.bitwise_and, r=["E1"], w=["E2"])
+        cp(T.YE[:, 64 * b:64 * b + 64], T.E2[:], ["E2"], [("YE", b)])
+
+    def step(t):
+        b, i, par, q = t // NS, t % NS, t % 2, table(t)
+        o = 1024 * par
+        end = t == B * NS - 1
+        win = T["TAB%d" % q][:, 0:NV] if b == 0 else T["SL%d" % q][:]
+        wtok = [("slab", q)] if b == 0 else [("sl", q, 0), ("sl", q, 1)]
+        prev = t > 0
+        cut = 8 - FIRST[t - 1]
+        if t == NS:
+            acopy(t - 1, 1)
+            acopy(t - 1, 0)
+            lacc(t - 2, 0, 8 - FIRST[t - 2])
+        if prev and not end:
+            lmul(t - 1, cut, 8)
+            lacc(t - 1, cut, 8)
+        usrc, utok = (T.EN[:, 64 * b:64 * b + 64], "EN") if i == 0 else (T.U[:, 64 * par:64 * par + 64], ("U", par))
+
+        def prod(c):
+            sw = T["TAB%d" % q][:, NV:NV + NE].indirect(T.EI[:, 64 * par + 16 * c:64 * par + 16 * c + 16])
+            tt(T.PR[:, CH * c:CH * c + CH], sw, T.A[:, o + CH * c:o + CH * c + CH], Op.mult,
+               [("spow", q), ("EI", par), ("A", par, c)], [("PR", c)])
+
+        for c in range(4):
+            act(T.A[:, o + CH * c:o + CH * c + CH], win.indirect(T.VI[:, 64 * par + 16 * c:64 * par + 16 * c + 16]), Fn.Copy,
+                wtok + [("VI", par)], [("A", par, c)])
+            if end:
+                lmul(t - 1, 2 * c, 2 * c + 2)
+                lacc(t - 1, 2 * c, 2 * c + 2)
+                lmul(t, 2 * c, 2 * c + 2)
+                lacc(t, 2 * c, 2 * c + 2, True)
+            else:
+                prod(c)
+            if c % 2 == 1 and t != NS - 1:
+                acopy(t, c // 2)
+        if end:
+            for h in range(2):
+                act(T.YL[:, 512 * h:512 * h + 512], PS[LB[h]][:], Fn.Exp, (), [("YL", h)], [LB[h]], scale=-1.0 / 128)
+                op("y", lambda: g.sync.dma_start(T.yl[:, 512 * h:512 * h + 512], T.YL[:, 512 * h:512 * h + 512]),
+                   [("YL", h)], (), dma=True)
+            for c in range(4):
+                prod(c)
+        mm([(PS[PA][:, 0:64], T.W[:, 15 - r:143 - r], T.PR[:, r::16], r == 0, r == 15) for r in range(16)],
+           ["W"] + [("PR", c) for c in range(4)], [PA])
+        if prev and i < NS - 1:
+            lmul(t - 1, 0, cut)
+            lacc(t - 1, 0, cut)
+        if t < NS and REORDER[t]:
+            c0 = sum(REORDER[:t])
+            c1 = c0 + REORDER[t]
+            act(T.AC[:, 16 * c0:16 * c1], TAB[:, 0:NV].indirect(T.CU[:, c0:c1]), Fn.Identity,
+                [("slab", rank), "CU"], ["AC"], bias=-15.0)
+        if BY_SCALAR[t]:
+            n = 128 * BY_SCALAR[t]
+            act(T.K[:, o:o + n], T["TAB%d" % q][:, NV + NE:].indirect(T.EI[:, 64 * par:64 * par + n // 16]), Fn.Copy,
+                [("kap", q), ("EI", par)], [("K", par)])
+        if t < NS and SCATTER[t]:
+            c0 = sum(SCATTER[:t])
+            c1 = c0 + SCATTER[t]
+            act(T.INVW[:].indirect(T.PU[:, c0:c1]), T.IOT[:, 16 * c0:16 * c1], Fn.Silu,
+                ["PU", ("IOT", 0)] + ([("IOT", 1)] if c1 > IOT0 else []), ["INVW"])
+            if c1 == 128:
+                op("y", lambda: g.sync.dma_start(T.INVL[:], T.INVW[0::16, :]), ["INVW"], ["INVL"], dma=True)
+        d = PS[PA][:, 0:64]
+        unew = T.U[:, 64 * (1 - par):64 * (1 - par) + 64]
+        if i < NS - 1:
+            ts(T.Q[:], d, -0.005, Op.mult, 5.4975, Op.add, w=["Q"], b=[PA])
+            m, md = PS[PA][:, 64:128], PS[PA][:, 128:192]
+            ts(m, T.Q[:], 0.5, Op.max, 2.0, Op.min, r=["Q"], w=["PM"], b=[PA])
+            tt(md, m, T.D2[:, 64 * b:64 * b + 64], Op.mult, ["PM", "D2"], ["PD"], [PA])
+            tt(T.Z[:], md, T.ZW[:], Op.add, ["PD", "ZW"], ["Z"], [PA])
+            voxel(1 - par)
+            tt(unew, usrc, d, Op.subtract, [utok], [("U", 1 - par)], [PA])
+            wrap()
+            record(1 - par, unew, ("U", 1 - par))
+            if b == 0 and i % S == S - 2:
+                j = i // S
+                ts(T.KM[:, 128 * j:128 * j + 64], T.V[:], float(P), Op.is_lt, r=["V"], w=[("KM", j, 0)])
+                ts(T.KM[:, 128 * j + 64:128 * j + 128], T.V[:], float(P), Op.is_ge, r=["V"], w=[("KM", j, 1)])
+            if t == NS - 3:
+                ts(T.NF[:], T.FM[:], -1.0, Op.mult, r=["FM"], w=["NF"])
+            if t == NS - 2:
+                tt(T.UF[:], unew, T.NF[:], Op.add, [("U", 1 - par), "NF"], ["UF"])
+        elif end:
+            tt(unew, usrc, d, Op.subtract, [utok], [("U", 1 - par)], [PA])
+            energies(b, unew, ("U", 1 - par))
+            op("y", lambda: g.sync.dma_start(T.ye[:], T.YE[:]), [("YE", 0), ("YE", 1)], (), dma=True)
+        else:
+            mend(t, usrc, utok, unew, d)
+
+    def mend(t, usrc, utok, unew, d):
+        par = t % 2
+        z = PS[PA][:, 64:128]
+        tt(z, T.UF[:], d, Op.subtract, ["UF"], ["PM"], [PA])
+        tt(T.Z2[:], z, T.NF[:], Op.max, ["PM", "NF"], ["Z2"], [PA])
+        ts(T.SG[:], T.Z2[:], -1.0, Op.max, 1.0, Op.min, r=["Z2"], w=["SG"])
+        mm([(PS[PB][:, 64 * h:64 * h + 64], T.M2[:], T.SG[:], True, True) for h in range(2)], ["M2", "SG"], [PB])
+        tt(unew, usrc, d, Op.subtract, [utok], [("U", 1 - par)], [PA])
+        for j in (1, 2, 3):
+            tt(T.TY[:, 128 * j:128 * j + 128], PS[PB][:, 0:128], T.KM[:, 128 * j:128 * j + 128], Op.mult,
+               [("KM", j, 0), ("KM", j, 1)], [("TY", j)], [PB])
+        ts(T.TO[:, 128:512], T.TY[:, 128:512], -1.0, Op.max, 1.0, Op.min, r=[("TY", j) for j in (1, 2, 3)], w=["TO"])
+        trs, tot = [], 0
+        for j in range(1, N):
+            dd = (rank + j) % N
+            rid, pid = topo.addr(cores[dd], core)
+            trs.append(RemoteDMATransfer(dst_ids=[DstId(rid=rid, pnc=pid)], dma_engine_mask=bits(verdict_lane(rank, dd)),
+                                         remote_sem=T.sem.tm, src=T.TO[:, 128 * j:128 * j + 128], dst=T.TL[:, 128 * j:128 * j + 128]))
+            tot += len(verdict_lane(rank, dd))
+        op("g", lambda: g.remote_dma_fused(trs, local_sem=T.sem.sent), ["TO"], (), remote=tot)
+        tt(T.TY[:, 0:128], PS[PB][:, 0:128], T.KM[:, 0:128], Op.mult, [("KM", 0, 0), ("KM", 0, 1)], [("TY", 0)], [PB])
+        lmul(t - 1, 0, 8 - FIRST[t - 1])
+        for c in (2, 3, 0, 1):
+            mm([(PS[AB[c]][:], T.ZB[:, 0:128], T.ZB[:], True, False)]
+               + [(PS[AB[c]][:, 128 * k:128 * k + 128], T.IDB[:], T.AC[:, 4 * c + k::16], False, False) for k in range(4)],
+               ["ZB", "IDB", "AC"], [AB[c]])
+        ts(T.TO[:, 0:128], T.TY[:, 0:128], -1.0, Op.max, 1.0, Op.min, r=[("TY", 0)], w=["T0"])
+        ts(T.INVU[:], T.INVL[:], 0.25 - IOFF, Op.add, r=["INVL"], w=["INVU"])
+        ts(T.MN[:, 0:128], T.TO[:, 0:128], 0.0, Op.min, r=["T0"], w=[("MN", 0)])
+        begin(1)
+        energies(0, unew, ("U", 1 - par))
+        tj = [T.TO[:, 0:128]] + [T.TL[:, 128 * j:128 * j + 128] for j in range(1, N)]
+
+        def total(k, col, js):
+            return [(PS[k][:, 128 * col:128 * col + 128], T.IDB[:], tj[j], n == 0, n == len(js) - 1) for n, j in enumerate(js)]
+
+        def least(name, n, k, col):
+            tt(T[name][:, 128 * n + 128:128 * n + 256], PS[k][:, 128 * col:128 * col + 128], T[name][:, 128 * n:128 * n + 128],
+               Op.min, [(name, n)], [(name, n + 1)], [k])
+
+        mm(total(PA, 0, (0, 1)) + total(PA, 1, (0, 1, 2)), ["IDB", "T0", "TL"], [PA])
+        mm(total(PB, 0, (0, 1, 2, 3)) + total(PB, 1, (2, 3)), ["IDB", "T0", "TL"], [PB])
+        ts(T.HM[:, 0:128], tj[3], 0.0, Op.min, r=["TL"], w=[("HM", 0)])
+        least("MN", 0, PA, 0)
+        least("MN", 1, PA, 1)
+        mm(total(PA, 2, (1, 2, 3)), ["IDB", "TL"], [PA])
+        least("HM", 0, PB, 1)
+        least("MN", 2, PB, 0)
+        least("HM", 1, PB, 0)
+        cp(T.SS[:], PS[PB][:, 0:128], (), ["SS"], [PB])
+        least("HM", 2, PA, 2)
+        mn, hm = T.MN[:, 384:512], T.HM[:, 384:512]
+        hb = (PA, AB[0], AB[1], AB[2])
+        yb = (PB, PA, PB, AB[0])
+        for c in range(4):
+            rs = range(4 * c, 4 * c + 4)
+            br = [("BR", r) for r in rs]
+
+            def lhs(r):
+                return T.BR[:, 128 * r:128 * r + 128]
+
+            def col(k, r):
+                return PS[k][:, 128 * (r % 4):128 * (r % 4) + 128]
+
+            mm([(col(AB[c], r), lhs(r), mn, False, r % 4 == 3) for r in rs], br + [("MN", 3)], [AB[c]])
+            act(T.CS[:, 512 * c:512 * c + 512], PS[AB[c]][:], Fn.Identity, (), [("CS", c)], [AB[c]], bias=225.0, scale=16.0)
+            mm([(col(hb[c], r), lhs(r), hm, True, True) for r in rs], br + [("HM", 3)], [hb[c]])
+            seq = []
+            for r in rs:
+                seq += [(col(yb[c], r), T.IDB[:], T.AC[:, r::16], True, False), (col(yb[c], r), lhs(r), T.SS[:], False, True)]
+            mm(seq, br + ["SS", "IDB", "AC"], [yb[c]])
+            qq = T.QQ[:, 512 * (c % 2):512 * (c % 2) + 512]
+            tt(qq, PS[hb[c]][:], T.CS[:, 512 * c:512 * c + 512], Op.min, [("CS", c)], [("QQ", c % 2)], [hb[c]])
+            tt(T.R[:, 512 * c:512 * c + 512], PS[yb[c]][:], qq, Op.min, [("QQ", c % 2)], [("R", c)], [yb[c]])
+        SL = T["SL%d" % rank]
+        rr = [("R", c) for c in range(4)] + ["INVU"]
+        act(SL[:, 0:1024], T.R[:].indirect(T.INVU[:, 0:64]), Fn.Relu, rr, [("sl", rank, 0)], bias=15.0)
+        ts(SL[:, 1024:], T.R[:].indirect(T.INVU[:, 64:128]), 15.0, Op.add, 0.0, Op.max, r=rr, w=[("sl", rank, 1)])
+        send(direct, SL[:], SL[:], "sl%d" % rank, [("sl", rank, 0), ("sl", rank, 1)])
+        for q, dd in passes:
+            send([dd], T["SL%d" % q][:], T["SL%d" % q][:], "sl%d" % q, [("sl", q, 0)])
+
+    for t in range(B * NS):
+        step(t)
+    for sem in sorted(count):
+        wait("g", (sem, count[sem], {}, "x"))

@@ -7,10 +7,12 @@ CH = 256
 YS = 13
 IOFF = 32
 IOT0 = 32
-BY_SCALAR = [0] + [6] * 10 + [8] * 12 + [0]
-FIRST = [2] + [3] * 9 + [1] + [3] * 13
-SCATTER = [20] + [12] * 9 + [0] * 2
-REORDER = [0] * 10 + [32, 96]
+BY_SCALAR = [0] + [3] * 10 + [4] * 12 + [0]
+SCATTER = [2, 6] + [6, 8] * 3 + [6] * 13 + [0] * 3
+REORDER = [0] * 21 + [16, 16, 96]
+ORDER = "quLmPdPzPPfwLveLiL"
+AW = 1
+WIDE = 1
 
 SCRATCH = {
     "PX": ("sbuf", [128, 128], "int32"), "PY": ("sbuf", [128, 128], "int32"), "VX": ("sbuf", [128, 128], "int32"),
@@ -238,25 +240,39 @@ def rank_program(g, core, T, topo):
     for k in range(16):
         act(T.BR[:, 128 * k:128 * k + 128], T.BD[:], Fn.Copy, ["BD", "SEL"], [("BR", k)], scale=T.SEL[:, k:k + 1])
 
-    def voxel(par):
-        ts(T.XH[:], T.Z[:], 4, Op.arith_shift_right, 63, Op.bitwise_and, r=["Z"], w=["XH"])
-        ts(T.YH[:], T.Z[:], YS - 2, Op.arith_shift_right, 31 << 6, Op.bitwise_and, r=["Z"], w=["YH"])
-        tt(T.V[:], T.XH[:], T.YH[:], Op.add, ["XH", "YH"], ["V"])
-        cp(T.VI[:, 64 * par:64 * par + 64], T.V[:], ["V"], [("VI", par)])
+    def cols(hs, o=0):
+        return slice(o + 32 * hs[0], o + 32 * hs[-1] + 32)
 
-    def record(par, src, tok):
-        ts(T.EI[:, 64 * par:64 * par + 64], src, 1.0 / 64, Op.mult, -31.5 / 64, Op.add, r=[tok], w=[("EI", par)])
+    def toks(name, hs):
+        return [(name, h) for h in hs]
 
-    def wrap():
-        ts(T.ZW[:], T.Z[:], (511 << YS) | 1023, Op.bitwise_and, r=["Z"], w=["ZW"])
+    def fields(hs):
+        c = cols(hs)
+        ts(T.XH[:, c], T.Z[:, c], 4, Op.arith_shift_right, 63, Op.bitwise_and, r=toks("Z", hs), w=toks("XH", hs))
+        ts(T.YH[:, c], T.Z[:, c], YS - 2, Op.arith_shift_right, 31 << 6, Op.bitwise_and, r=toks("Z", hs), w=toks("YH", hs))
+
+    def voxel(hs):
+        c = cols(hs)
+        tt(T.V[:, c], T.XH[:, c], T.YH[:, c], Op.add, toks("XH", hs) + toks("YH", hs), toks("V", hs))
+
+    def listed(par, hs):
+        cp(T.VI[:, cols(hs, 64 * par)], T.V[:, cols(hs)], toks("V", hs), [("VI", par, h) for h in hs])
+
+    def record(par, hs, src, tok):
+        ts(T.EI[:, cols(hs, 64 * par)], src, 1.0 / 64, Op.mult, -31.5 / 64, Op.add, r=[tok], w=[("EI", par, h) for h in hs])
+
+    def wrap(hs):
+        ts(T.ZW[:, cols(hs)], T.Z[:, cols(hs)], (511 << YS) | 1023, Op.bitwise_and, r=toks("Z", hs), w=toks("ZW", hs))
 
     def begin(b):
-        c = slice(64 * b, 64 * b + 64)
+        c, hs = slice(64 * b, 64 * b + 64), [0, 1]
         ts(T.MD[:], T.PY[:, c], float(1 << YS), Op.mult, r=["PY"], w=["MD"])
-        tt(T.Z[:], T.MD[:], T.PX[:, c], Op.add, ["MD", "PX"], ["Z"])
-        voxel(0)
-        record(0, T.EN[:, c], "EN")
-        wrap()
+        record(0, hs, T.EN[:, c], "EN")
+        tt(T.Z[:], T.MD[:], T.PX[:, c], Op.add, ["MD", "PX"], toks("Z", hs))
+        fields(hs)
+        wrap(hs)
+        voxel(hs)
+        listed(0, hs)
 
     begin(0)
     ts(T.I1[:], T.COR[:], 15, Op.bitwise_and, r=["COR"], w=["I1"])
@@ -274,143 +290,185 @@ def rank_program(g, core, T, topo):
     def table(t):
         return (rank + (t % NS) // S) % N
 
-    def lmul(t, u0, u1):
-        par, q, nx = t % 2, table(t), BY_SCALAR[t]
-        o = 1024 * par
-        u = u0
-        while u < u1:
-            if u < nx:
-                e = min(u1, nx, u // 4 * 4 + 4)
-                k = AB[2 * par + u // 4]
-                tt(T.AK[:, o + 128 * u:o + 128 * e], PS[k][:, 128 * (u % 4):128 * (u % 4 + e - u)], T.K[:, o + 128 * u:o + 128 * e],
-                   Op.mult, [("K", par)], [("AK", par, i) for i in range(u, e)], [k])
-            else:
-                e = u1
-                win = T["TAB%d" % q][:, NV + NE:].indirect(T.EI[:, 64 * par + 8 * u:64 * par + 8 * e])
-                tt(T.AK[:, o + 128 * u:o + 128 * e], win, T.A[:, o + 128 * u:o + 128 * e], Op.mult,
-                   [("kap", q), ("EI", par)] + [("A", par, i // 2) for i in range(u, e)], [("AK", par, i) for i in range(u, e)])
-            u = e
-
-    def lacc(t, u0, u1, last=False):
-        o = 1024 * (t % 2)
-        u = u0
-        while u < u1:
-            e = min(u1, u // 4 * 4 + 4)
-            mm([(PS[LB[u // 4]][:, 128 * (u % 4):128 * (u % 4 + e - u)], T.IDF[:], T.AK[:, o + 128 * u:o + 128 * e], False,
-                 last and e % 4 == 0)], ["IDF"] + [("AK", t % 2, i) for i in range(u, e)], [LB[u // 4]])
-            u = e
+    def lmul(t, h, u):
+        par, q, x = t % 2, table(t), 4 * h + u
+        o = 1024 * par + 128 * x
+        if u < BY_SCALAR[t]:
+            k = AB[2 * par + h]
+            tt(T.AK[:, o:o + 128], PS[k][:, 128 * u:128 * u + 128], T.K[:, o:o + 128], Op.mult, [("K", par, h)], [("AK", par, x)], [k])
+        else:
+            win = T["TAB%d" % q][:, NV + NE:].indirect(T.EI[:, 64 * par + 8 * x:64 * par + 8 * x + 8])
+            tt(T.AK[:, o:o + 128], win, T.A[:, o:o + 128], Op.mult, [("kap", q), ("EI", par, h), ("A", par, x)], [("AK", par, x)])
 
     def acopy(t, h):
-        par, n = t % 2, 128 * min(4, BY_SCALAR[t] - 4 * h)
+        par, n = t % 2, 128 * BY_SCALAR[t]
         if n > 0:
             k, o = AB[2 * par + h], 1024 * par + 512 * h
-            mm([(PS[k][:, 0:n], T.IDB[:], T.A[:, o:o + n], True, True)], ["IDB", ("A", par, 2 * h), ("A", par, 2 * h + 1)], [k])
+            mm([(PS[k][:, 0:n], T.IDB[:], T.A[:, o:o + n], True, True)], ["IDB"] + [("A", par, 4 * h + x) for x in range(4)], [k])
 
-    def energies(b, src, tok):
-        ts(T.E1[:], src, 0.0, Op.max, r=[tok], w=["E1"])
+    def energies(b, t):
+        n = 1 - t % 2
+        ts(T.E1[:], T.U[:, 64 * n:64 * n + 64], 0.0, Op.max, r=[("U", n, 0), ("U", n, 1)], w=["E1"])
         ts(T.E2[:], T.E1[:], 1023, Op.bitwise_and, r=["E1"], w=["E2"])
         cp(T.YE[:, 64 * b:64 * b + 64], T.E2[:], ["E2"], [("YE", b)])
 
     def step(t):
-        b, i, par, q = t // NS, t % NS, t % 2, table(t)
-        o = 1024 * par
-        end = t == B * NS - 1
-        win = T["TAB%d" % q][:, 0:NV] if b == 0 else T["SL%d" % q][:]
-        wtok = [("slab", q)] if b == 0 else [("sl", q, 0), ("sl", q, 1)]
-        prev = t > 0
-        cut = 8 - FIRST[t - 1]
-        if t == NS:
-            acopy(t - 1, 1)
-            acopy(t - 1, 0)
-            lacc(t - 2, 0, 8 - FIRST[t - 2])
-        if prev and not end:
-            lmul(t - 1, cut, 8)
-            lacc(t - 1, cut, 8)
-        usrc, utok = (T.EN[:, 64 * b:64 * b + 64], "EN") if i == 0 else (T.U[:, 64 * par:64 * par + 64], ("U", par))
-
-        def prod(c):
-            sw = T["TAB%d" % q][:, NV:NV + NE].indirect(T.EI[:, 64 * par + 16 * c:64 * par + 16 * c + 16])
-            tt(T.PR[:, CH * c:CH * c + CH], sw, T.A[:, o + CH * c:o + CH * c + CH], Op.mult,
-               [("spow", q), ("EI", par), ("A", par, c)], [("PR", c)])
-
-        for c in range(4):
-            act(T.A[:, o + CH * c:o + CH * c + CH], win.indirect(T.VI[:, 64 * par + 16 * c:64 * par + 16 * c + 16]), Fn.Copy,
-                wtok + [("VI", par)], [("A", par, c)])
-            if end:
-                lmul(t - 1, 2 * c, 2 * c + 2)
-                lacc(t - 1, 2 * c, 2 * c + 2)
-                lmul(t, 2 * c, 2 * c + 2)
-                lacc(t, 2 * c, 2 * c + 2, True)
-            else:
-                prod(c)
-            if c % 2 == 1 and t != NS - 1:
-                acopy(t, c // 2)
-        if end:
-            for h in range(2):
-                act(T.YL[:, 512 * h:512 * h + 512], PS[LB[h]][:], Fn.Exp, (), [("YL", h)], [LB[h]], scale=-1.0 / 128)
-                op("y", lambda: g.sync.dma_start(T.yl[:, 512 * h:512 * h + 512], T.YL[:, 512 * h:512 * h + 512]),
-                   [("YL", h)], (), dma=True)
+        if t % NS == 0:
+            gather(t, 0)
+            gather(t, 1)
             for c in range(4):
-                prod(c)
-        mm([(PS[PA][:, 0:64], T.W[:, 15 - r:143 - r], T.PR[:, r::16], r == 0, r == 15) for r in range(16)],
-           ["W"] + [("PR", c) for c in range(4)], [PA])
-        if prev and i < NS - 1:
-            lmul(t - 1, 0, cut)
-            lacc(t - 1, 0, cut)
-        if t < NS and REORDER[t]:
-            c0 = sum(REORDER[:t])
-            c1 = c0 + REORDER[t]
+                prod(t, 0, c)
+            losses(t, 0)
+            after(t, 0)
+        if t == NS:
+            acopy(t - 1, 0)
+            acopy(t - 1, 1)
+            later.extend((t - 1, h) for h in range(2))
+        phase(t, 0, (t, 1))
+        if t == NS - 1:
+            phase(t, 1, None)
+            mend(t)
+        elif t == B * NS - 1:
+            phase(t, 1, None)
+            energies(1, t)
+            op("y", lambda: g.sync.dma_start(T.ye[:], T.YE[:]), [("YE", 0), ("YE", 1)], (), dma=True)
+        else:
+            phase(t, 1, (t + 1, 0))
+
+    later = []
+
+    def gather(t, h):
+        par, q = t % 2, table(t)
+        win = T["TAB%d" % q][:, 0:NV] if t < NS else T["SL%d" % q][:]
+        wtok = [("slab", q)] if t < NS else [("sl", q, 0), ("sl", q, 1)]
+        for u in range(4 * h, 4 * h + 4, AW):
+            o = 1024 * par + 128 * u
+            act(T.A[:, o:o + 128 * AW], win.indirect(T.VI[:, 64 * par + 8 * u:64 * par + 8 * (u + AW)]), Fn.Copy,
+                wtok + [("VI", par, h)], [("A", par, u + x) for x in range(AW)])
+
+    def prod(t, h, c):
+        par, q, u = t % 2, table(t), 4 * h + c
+        if WIDE > 1:
+            if c % WIDE:
+                return
+        sw = T["TAB%d" % q][:, NV:NV + NE].indirect(T.EI[:, 64 * par + 8 * u:64 * par + 8 * (u + WIDE)])
+        o = 1024 * par + 128 * u
+        tt(T.PR[:, 128 * u:128 * (u + WIDE)], sw, T.A[:, o:o + 128 * WIDE], Op.mult,
+           [("spow", q), ("EI", par, h)] + [("A", par, u + i) for i in range(WIDE)], [("PR", u + i) for i in range(WIDE)])
+
+    def losses(t, h):
+        k = (PA, PB)[h]
+        mm([(PS[k][:, 0:32], T.W[:, 15 - r:143 - r], T.PR[:, 512 * h + r:512 * h + 512:16], r == 0, r == 15) for r in range(16)],
+           ["W"] + [("PR", 4 * h + c) for c in range(4)], [k])
+
+    def after(t, h):
+        par, q, ph = t % 2, table(t), 2 * t + h
+        if t != NS - 1:
+            acopy(t, h)
+        if t < NS and REORDER[ph]:
+            c0 = sum(REORDER[:ph])
+            c1 = c0 + REORDER[ph]
             act(T.AC[:, 16 * c0:16 * c1], TAB[:, 0:NV].indirect(T.CU[:, c0:c1]), Fn.Identity,
                 [("slab", rank), "CU"], ["AC"], bias=-15.0)
         if BY_SCALAR[t]:
-            n = 128 * BY_SCALAR[t]
-            act(T.K[:, o:o + n], T["TAB%d" % q][:, NV + NE:].indirect(T.EI[:, 64 * par:64 * par + n // 16]), Fn.Copy,
-                [("kap", q), ("EI", par)], [("K", par)])
-        if t < NS and SCATTER[t]:
-            c0 = sum(SCATTER[:t])
-            c1 = c0 + SCATTER[t]
+            n, o, c = 128 * BY_SCALAR[t], 1024 * par + 512 * h, 64 * par + 32 * h
+            act(T.K[:, o:o + n], T["TAB%d" % q][:, NV + NE:].indirect(T.EI[:, c:c + n // 16]), Fn.Copy,
+                [("kap", q), ("EI", par, h)], [("K", par, h)])
+        if t < NS and SCATTER[ph]:
+            c0 = sum(SCATTER[:ph])
+            c1 = c0 + SCATTER[ph]
             act(T.INVW[:].indirect(T.PU[:, c0:c1]), T.IOT[:, 16 * c0:16 * c1], Fn.Silu,
                 ["PU", ("IOT", 0)] + ([("IOT", 1)] if c1 > IOT0 else []), ["INVW"])
             if c1 == 128:
                 op("y", lambda: g.sync.dma_start(T.INVL[:], T.INVW[0::16, :]), ["INVW"], ["INVL"], dma=True)
-        d = PS[PA][:, 0:64]
-        unew = T.U[:, 64 * (1 - par):64 * (1 - par) + 64]
-        if i < NS - 1:
-            ts(T.Q[:], d, -0.005, Op.mult, 5.4975, Op.add, w=["Q"], b=[PA])
-            m, md = PS[PA][:, 64:128], PS[PA][:, 128:192]
-            ts(m, T.Q[:], 0.5, Op.max, 2.0, Op.min, r=["Q"], w=["PM"], b=[PA])
-            tt(md, m, T.D2[:, 64 * b:64 * b + 64], Op.mult, ["PM", "D2"], ["PD"], [PA])
-            tt(T.Z[:], md, T.ZW[:], Op.add, ["PD", "ZW"], ["Z"], [PA])
-            voxel(1 - par)
-            tt(unew, usrc, d, Op.subtract, [utok], [("U", 1 - par)], [PA])
-            wrap()
-            record(1 - par, unew, ("U", 1 - par))
+        if t != NS - 1:
+            later.append((t, h))
+
+    def phase(t, h, other):
+        b, i, par, k = t // NS, t % NS, t % 2, (PA, PB)[h]
+        end = t == B * NS - 1
+        c = slice(32 * h, 32 * h + 32)
+        d, m, md = PS[k][:, 0:32], PS[k][:, 64:96], PS[k][:, 128:160]
+        o, n = 64 * par + 32 * h, 64 * (1 - par) + 32 * h
+        usrc, utok = (T.EN[:, 64 * b + 32 * h:64 * b + 32 * h + 32], "EN") if i == 0 else (T.U[:, o:o + 32], ("U", par, h))
+        unew, ntok = T.U[:, n:n + 32], ("U", 1 - par, h)
+        todo = [later.pop(0) for _ in range(min(len(later), 2))]
+        pieces = [(x, u) for x in todo for u in range(4)]
+        if other and (i, h) != (0, 0):
+            gather(*other)
+
+        def big(cc):
+            if other:
+                prod(other[0], other[1], cc)
+                if cc == 3:
+                    losses(*other)
+                    after(*other)
+
+        def part(num):
+            for _ in range(num * len(todo)):
+                if pieces:
+                    (tt_, hh), u = pieces.pop(0)
+                    lmul(tt_, hh, u)
+                    if u == 3:
+                        last = tt_ == B * NS - 1
+                        mm([(PS[LB[hh]][:], T.IDF[:], T.AK[:, 1024 * (tt_ % 2) + 512 * hh:1024 * (tt_ % 2) + 512 * hh + 512], False, last)],
+                           ["IDF"] + [("AK", tt_ % 2, 4 * hh + x) for x in range(4)], [LB[hh]])
+                        if last:
+                            act(T.YL[:, 512 * hh:512 * hh + 512], PS[LB[hh]][:], Fn.Exp, (), [("YL", hh)], [LB[hh]], scale=-1.0 / 128)
+                            op("y", lambda: g.sync.dma_start(T.yl[:, 512 * hh:512 * hh + 512], T.YL[:, 512 * hh:512 * hh + 512]),
+                               [("YL", hh)], (), dma=True)
+
+        if end:
+            part(4)
+            for cc in range(4):
+                big(cc)
+            tt(unew, usrc, d, Op.subtract, [utok], [ntok], [k])
+        elif i == NS - 1:
+            tt(m, T.UF[:, c], d, Op.subtract, [("UF", h)], [("PM", h)], [k])
+            big(0)
+            tt(T.Z2[:, c], m, T.NF[:, c], Op.max, [("PM", h), "NF"], [("Z2", h)], [k])
+            tt(unew, usrc, d, Op.subtract, [utok], [ntok], [k])
+            big(1)
+            big(2)
+            ts(T.SG[:, c], T.Z2[:, c], -1.0, Op.max, 1.0, Op.min, r=[("Z2", h)], w=[("SG", h)])
+            big(3)
+            part(4)
+        else:
+            nbig = [0]
+
+            def products():
+                big(nbig[0])
+                nbig[0] += 1
+
+            calls = {
+                "q": lambda: ts(T.Q[:, c], d, -0.005, Op.mult, 5.4975, Op.add, w=[("Q", h)], b=[k]),
+                "m": lambda: ts(m, T.Q[:, c], 0.5, Op.max, 2.0, Op.min, r=[("Q", h)], w=[("PM", h)], b=[k]),
+                "d": lambda: tt(md, m, T.D2[:, 64 * b + 32 * h:64 * b + 32 * h + 32], Op.mult, [("PM", h), "D2"], [("PD", h)], [k]),
+                "z": lambda: tt(T.Z[:, c], md, T.ZW[:, c], Op.add, [("PD", h), ("ZW", h)], [("Z", h)], [k]),
+                "f": lambda: fields([h]), "v": lambda: voxel([h]), "i": lambda: listed(1 - par, [h]),
+                "u": lambda: tt(unew, usrc, d, Op.subtract, [utok], [ntok], [k]),
+                "e": lambda: record(1 - par, [h], unew, ntok), "w": lambda: wrap([h]),
+                "P": products, "L": lambda: part(1),
+            }
+            for x in ORDER:
+                calls[x]()
             if b == 0 and i % S == S - 2:
-                j = i // S
-                ts(T.KM[:, 128 * j:128 * j + 64], T.V[:], float(P), Op.is_lt, r=["V"], w=[("KM", j, 0)])
-                ts(T.KM[:, 128 * j + 64:128 * j + 128], T.V[:], float(P), Op.is_ge, r=["V"], w=[("KM", j, 1)])
-            if t == NS - 3:
+                j = 128 * (i // S) + 32 * h
+                ts(T.KM[:, j:j + 32], T.V[:, c], float(P), Op.is_lt, r=[("V", h)], w=[("KM", i // S, 0, h)])
+                ts(T.KM[:, j + 64:j + 96], T.V[:, c], float(P), Op.is_ge, r=[("V", h)], w=[("KM", i // S, 1, h)])
+            if t == NS - 3 and h == 0:
                 ts(T.NF[:], T.FM[:], -1.0, Op.mult, r=["FM"], w=["NF"])
             if t == NS - 2:
-                tt(T.UF[:], unew, T.NF[:], Op.add, [("U", 1 - par), "NF"], ["UF"])
-        elif end:
-            tt(unew, usrc, d, Op.subtract, [utok], [("U", 1 - par)], [PA])
-            energies(b, unew, ("U", 1 - par))
-            op("y", lambda: g.sync.dma_start(T.ye[:], T.YE[:]), [("YE", 0), ("YE", 1)], (), dma=True)
-        else:
-            mend(t, usrc, utok, unew, d)
+                tt(T.UF[:, c], unew, T.NF[:, c], Op.add, [ntok, "NF"], [("UF", h)])
 
-    def mend(t, usrc, utok, unew, d):
-        par = t % 2
-        z = PS[PA][:, 64:128]
-        tt(z, T.UF[:], d, Op.subtract, ["UF"], ["PM"], [PA])
-        tt(T.Z2[:], z, T.NF[:], Op.max, ["PM", "NF"], ["Z2"], [PA])
-        ts(T.SG[:], T.Z2[:], -1.0, Op.max, 1.0, Op.min, r=["Z2"], w=["SG"])
-        mm([(PS[PB][:, 64 * h:64 * h + 64], T.M2[:], T.SG[:], True, True) for h in range(2)], ["M2", "SG"], [PB])
-        tt(unew, usrc, d, Op.subtract, [utok], [("U", 1 - par)], [PA])
+    def band(j):
+        return [("KM", j, x, h) for x in range(2) for h in range(2)]
+
+    def mend(t):
+        mm([(PS[PB][:, 64 * h:64 * h + 64], T.M2[:], T.SG[:], True, True) for h in range(2)], ["M2", ("SG", 0), ("SG", 1)], [PB])
         for j in (1, 2, 3):
             tt(T.TY[:, 128 * j:128 * j + 128], PS[PB][:, 0:128], T.KM[:, 128 * j:128 * j + 128], Op.mult,
-               [("KM", j, 0), ("KM", j, 1)], [("TY", j)], [PB])
+               band(j), [("TY", j)], [PB])
         ts(T.TO[:, 128:512], T.TY[:, 128:512], -1.0, Op.max, 1.0, Op.min, r=[("TY", j) for j in (1, 2, 3)], w=["TO"])
         trs, tot = [], 0
         for j in range(1, N):
@@ -420,8 +478,7 @@ def rank_program(g, core, T, topo):
                                          remote_sem=T.sem.tm, src=T.TO[:, 128 * j:128 * j + 128], dst=T.TL[:, 128 * j:128 * j + 128]))
             tot += len(verdict_lane(rank, dd))
         op("g", lambda: g.remote_dma_fused(trs, local_sem=T.sem.sent), ["TO"], (), remote=tot)
-        tt(T.TY[:, 0:128], PS[PB][:, 0:128], T.KM[:, 0:128], Op.mult, [("KM", 0, 0), ("KM", 0, 1)], [("TY", 0)], [PB])
-        lmul(t - 1, 0, 8 - FIRST[t - 1])
+        tt(T.TY[:, 0:128], PS[PB][:, 0:128], T.KM[:, 0:128], Op.mult, band(0), [("TY", 0)], [PB])
         for c in (2, 3, 0, 1):
             mm([(PS[AB[c]][:], T.ZB[:, 0:128], T.ZB[:], True, False)]
                + [(PS[AB[c]][:, 128 * k:128 * k + 128], T.IDB[:], T.AC[:, 4 * c + k::16], False, False) for k in range(4)],
@@ -430,7 +487,7 @@ def rank_program(g, core, T, topo):
         ts(T.INVU[:], T.INVL[:], 0.25 - IOFF, Op.add, r=["INVL"], w=["INVU"])
         ts(T.MN[:, 0:128], T.TO[:, 0:128], 0.0, Op.min, r=["T0"], w=[("MN", 0)])
         begin(1)
-        energies(0, unew, ("U", 1 - par))
+        energies(0, t)
         tj = [T.TO[:, 0:128]] + [T.TL[:, 128 * j:128 * j + 128] for j in range(1, N)]
 
         def total(k, col, js):

@@ -3,54 +3,69 @@ from concourse.mybir import AluOpType as Op, ActivationFunctionType as Fn
 
 N, NV, NE, P, S, B = 4, 2048, 1024, 1024, 3, 2
 NS = N * S
-CH = 256
-YS = 13
 IOFF = 32
-IOT0 = 32
-BY_SCALAR = [0] + [3] * 10 + [4] * 12 + [0]
-SCATTER = [2, 6] + [6, 8] * 3 + [6] * 13 + [0] * 3
-REORDER = [0] * 21 + [16, 16, 96]
-ORDER = "quLmPdPzPPfwLveLiL"
-AW = 1
-WIDE = 1
+PASS = 2
+IOT0 = 96
+ALPHA = 123 / 2 ** 14
+OH, OR = 24576, 16768
+SCATTER = [0, 40] + [4, 0, 0, 0] * 4 + [0] * 5 + [72]
+REORDER = [0] * 11 + [16, 0, 0] * 4 + [64]
+KPLAN = [0] * 2 + [1] * 21 + [3] + [1] * 24
+BY_DMA = [n for n in range(2, 19) if n % 8 not in (3, 6)] + list(range(19, 24)) + [n for n in range(27, 40) if n % 4 in (0, 3)]
+JOIN = [22]
+NACC = len(JOIN)
+RING = 12
+KR = 12
+SUMS = [0] * 4 + [1] * 17 + [0] * 4 + [1] * 23
+FUSED = [21, 22, 23]
+MENDL = 20
+GA = (128, 256, 128)
+LW = 128
+ORDER = "mWcPazPVaPLidLLLAAs"
+MEND = "Z0 H0 Z1 Y0 q0 Z2 H1 Y1 q1 r0 Z3 H2 Y2 q2 r1 H3 Y3 q3 r2 r3".split()
 
 SCRATCH = {
     "PX": ("sbuf", [128, 128], "int32"), "PY": ("sbuf", [128, 128], "int32"), "VX": ("sbuf", [128, 128], "int32"),
     "VY": ("sbuf", [128, 128], "int32"), "EN": ("sbuf", [128, 128], "int32"), "FM": ("sbuf", [128, 64], "int32"),
     "COR": ("sbuf", [128, 128], "int32"),
-    "IOI": ("sbuf", [128, 144], "int32"), "PCI": ("sbuf", [128, 4], "int32"), "PCF": ("sbuf", [128, 4], "float32"),
-    "W": ("sbuf", [128, 144], "bfloat16"), "IDB": ("sbuf", [128, 128], "bfloat16"), "IDF": ("sbuf", [128, 128], "float32"),
+    "IOI": ("sbuf", [128, 144], "int32"), "PCI": ("sbuf", [128, 4], "int32"), "PCF": ("sbuf", [128, 16], "float32"),
+    "WL": ("sbuf", [128, 144], "bfloat16"), "WY": ("sbuf", [128, 136], "bfloat16"), "GH": ("sbuf", [128, 136], "float16"),
+    "GR": ("sbuf", [128, 136], "float16"), "S0": ("sbuf", [128, 136], "float16"), "S1": ("sbuf", [128, 136], "float16"),
+    "IDB": ("sbuf", [128, 128], "bfloat16"), "IDF": ("sbuf", [128, 128], "float32"), "IDH": ("sbuf", [128, 128], "float16"),
+    "I8": ("sbuf", [128, 128], "bfloat16"), "I254": ("sbuf", [128, 128], "float16"),
+    "CK": ("sbuf", [128, 512], "bfloat16"), "ONE": ("sbuf", [128, 512], "bfloat16"),
     "ZB": ("sbuf", [128, 512], "bfloat16"), "BD": ("sbuf", [128, 128], "bfloat16"), "SEL": ("sbuf", [128, 16], "float32"),
     "M2": ("sbuf", [128, 128], "bfloat16"), "BR": ("sbuf", [128, 2048], "bfloat16"),
     "I1": ("sbuf", [128, 128], "int32"), "I2": ("sbuf", [128, 128], "int32"), "I3": ("sbuf", [128, 128], "int32"),
-    "F1": ("sbuf", [128, 128], "float32"), "F2": ("sbuf", [128, 128], "float32"), "H1": ("sbuf", [128, 128], "bfloat16"),
-    "D2": ("sbuf", [128, 128], "float32"),
-    "Z": ("sbuf", [128, 64], "int32"), "ZW": ("sbuf", [128, 64], "int32"), "Q": ("sbuf", [128, 64], "int32"),
-    "MD": ("sbuf", [128, 64], "float32"), "XH": ("sbuf", [128, 64], "int32"),
-    "YH": ("sbuf", [128, 64], "int32"), "V": ("sbuf", [128, 64], "int32"), "U": ("sbuf", [128, 128], "float32"),
-    "VI": ("sbuf", [128, 128], "uint16"), "EI": ("sbuf", [128, 128], "uint16"),
-    "A": ("sbuf", [128, 2048], "bfloat16"), "K": ("sbuf", [128, 2048], "bfloat16"), "PR": ("sbuf", [128, 1024], "bfloat16"),
-    "AK": ("sbuf", [128, 2048], "float32"),
+    "F1": ("sbuf", [128, 144], "float32"), "F2": ("sbuf", [128, 128], "float32"), "H1": ("sbuf", [128, 128], "bfloat16"),
+    "PH": ("sbuf", [128, 512], "float16"), "X0": ("sbuf", [128, 256], "float32"), "DH": ("sbuf", [128, 256], "float16"),
+    "XS": ("sbuf", [128, 192], "float32"), "D0": ("sbuf", [128, 384], "bfloat16"), "D1": ("sbuf", [128, 576], "float32"),
+    "SC": ("sbuf", [128, 768], "float16"), "CQ": ("sbuf", [128, 256], "bfloat16"),
+    "DR": ("sbuf", [128, 128], "float16"),
+    "IL": ("sbuf", [128, 128 * B * NS], "uint16"), "A": ("sbuf", [128, P * B * NS], "bfloat16"),
+    "K": ("sbuf", [128, 512 * KR], "bfloat16"), "PR": ("sbuf", [128, 1024], "bfloat16"), "AK": ("sbuf", [128, 2048], "float16"),
+    "LD": ("sbuf", [128, 1024 * NACC], "float32"),
+    "AD": ("sbuf", [128, 512 * RING], "float32"),
     "CU": ("sbuf", [128, 128], "uint16"), "PU": ("sbuf", [128, 128], "uint16"), "IOT": ("sbuf", [128, 2048], "float32"),
     "INVW": ("sbuf", [128, 2048], "float32"), "INVL": ("sbuf", [128, 128], "float32"), "INVU": ("sbuf", [128, 128], "uint16"),
-    "AC": ("sbuf", [128, 2048], "bfloat16"), "CS": ("sbuf", [128, 2048], "bfloat16"), "QQ": ("sbuf", [128, 1024], "bfloat16"),
+    "AC": ("sbuf", [128, 2048], "bfloat16"), "CS": ("sbuf", [128, 2048], "bfloat16"), "QQ": ("sbuf", [128, 2048], "bfloat16"),
     "R": ("sbuf", [128, 2048], "bfloat16"),
     "KM": ("sbuf", [128, 512], "bfloat16"), "TY": ("sbuf", [128, 512], "bfloat16"), "TO": ("sbuf", [128, 512], "bfloat16"),
-    "TL": ("sbuf", [128, 512], "bfloat16"), "UF": ("sbuf", [128, 64], "float32"), "NF": ("sbuf", [128, 64], "float32"),
+    "TL": ("sbuf", [128, 512], "bfloat16"), "NF": ("sbuf", [128, 64], "float32"),
     "Z2": ("sbuf", [128, 64], "float32"), "SG": ("sbuf", [128, 64], "bfloat16"),
     "MN": ("sbuf", [128, 512], "bfloat16"), "HM": ("sbuf", [128, 512], "bfloat16"), "SS": ("sbuf", [128, 128], "bfloat16"),
-    "E1": ("sbuf", [128, 64], "int32"), "E2": ("sbuf", [128, 64], "int32"), "YE": ("sbuf", [128, 128], "float32"),
-    "YL": ("sbuf", [128, 1024], "float32"),
+    "E0": ("sbuf", [128, 64], "float32"), "E1": ("sbuf", [128, 64], "int32"), "E2": ("sbuf", [128, 64], "int32"),
+    "YE": ("sbuf", [128, 128], "float32"), "YL": ("sbuf", [128, 1024], "float32"),
 }
 for _q in range(N):
     SCRATCH["TAB%d" % _q] = ("sbuf", [128, NV + 2 * NE], "bfloat16")
     SCRATCH["SL%d" % _q] = ("sbuf", [128, NV], "bfloat16")
-for _b in range(8):
-    SCRATCH["PS%d" % _b] = ("psum", [128, 512], "float32")
-SEMAPHORES = (["cv", "cs", "cp", "cg", "sent", "tm"] + [_p + str(_q) for _q in range(N) for _p in ("slab", "spow", "kap", "sl")]
-              + ["d%d" % _i for _i in range(14)])
+for _b in range(4):
+    SCRATCH["PS%d" % _b] = ("psum", [128, 1024], "float32")
+SEMAPHORES = (["cv", "cs", "cp", "cg", "sent", "tm"] + [_p + str(_q) for _q in range(N) for _p in ("slab", "spow", "kap", "sl", "fslab", "fspow", "fkap", "fsl")]
+              + ["d%d" % _i for _i in range(14 + len(BY_DMA))])
 
-LB, AB, PA, PB = (0, 1), (2, 3, 4, 5), 6, 7
+LB, AB, PB, QB = (0, 1), (2, 3), (5, 6), (4, 7)
 
 
 def bits(engines):
@@ -81,7 +96,7 @@ def rank_program(g, core, T, topo):
                 known[q][k] = x
 
     def op(q, fn, r=(), w=(), b=(), dma=False, remote=0):
-        need = [wrote[t] for t in r if t in wrote] + [wrote[t] for t in w if t in wrote]
+        need = [wrote[t] for t in r] + [wrote[t] for t in w if t in wrote]
         for t in w:
             need += read.get(t, [])
         for k in b:
@@ -131,6 +146,9 @@ def rank_program(g, core, T, topo):
     def cp(out, in_, r=(), w=(), b=()):
         op("v", lambda: g.vector.tensor_copy(out, in_), r, w, b)
 
+    def fill(out, x, w):
+        op("v", lambda: g.vector.memset(out, x), (), w)
+
     def act(out, in_, f, r=(), w=(), b=(), **kw):
         op("s", lambda: g.scalar.activation(out, in_, f, **kw), r, w, b)
 
@@ -142,7 +160,8 @@ def rank_program(g, core, T, topo):
             return ins
         op("p", run, r, (), b)
 
-    PS = [T["PS%d" % k] for k in range(8)]
+    def ps(k, c0=0, c1=512):
+        return T["PS%d" % (k // 2)][:, 512 * (k % 2) + c0:512 * (k % 2) + c1]
 
     def near(a, b):
         return cores[b] in topo.cores_of(cores[a])
@@ -160,17 +179,53 @@ def rank_program(g, core, T, topo):
         first = min((x for x in range(N) if near(x, d)), key=lambda x: (q - x) % N)
         return q if first == d else first
 
-    def lane(a, d):
-        return lanes(a)[1 if near(a, d) else 0]
+    def calls_of(a, parts):
+        mate = [d for d in range(N) if d != a and near(a, d)][0]
+        far = {q: [d for d in range(N) if not near(q, d) and source_of(q, d) == q][0] for q in (a, mate)}
+        off, on = lanes(a)
+        out = []
+        if (a - far[a]) % N == 1:
+            for part, c0, c1 in parts:
+                m = (c0 + c1) // 2
+                out.append([(far[a], a, part, c0, m, off, part), (mate, a, part, m, c1, on, "f" + part)])
+            for part, c0, c1 in parts:
+                m = (c0 + c1) // 2
+                out.append([(far[mate], mate, part, m, c1, off, part), (mate, a, part, c0, m, on, part)])
+        else:
+            out += [[(mate, a, part, c0, c1, off + on, part)] for part, c0, c1 in parts]
+            out += [[(far[mate], mate, part, (c0 + c1) // 2, c1, off, part)] for part, c0, c1 in parts]
+            out += [[(far[a], a, part, c0, (c0 + c1) // 2, off, part)] for part, c0, c1 in parts]
+        return out
 
-    def send(dests, src, dst, sem, r):
-        trs, tot = [], 0
-        for d in dests:
+    def passes_of(a, parts, j):
+        mate = [d for d in range(N) if d != a and near(a, d)][0]
+        q, (off, on) = (a + j) % N, lanes(a)
+        if near(a, q) or source_of(q, mate) != a:
+            return []
+        return [[(mate, q, part, c0, c1, on if j == 1 else off + on, part)] for part, c0, c1 in parts]
+
+    def expect(parts):
+        total = {}
+        for a in range(N):
+            for call in calls_of(a, parts) + [x for j in range(1, N) for x in passes_of(a, parts, j)]:
+                for d, q, part, c0, c1, es, sem in call:
+                    if d == rank:
+                        total[(sem, q)] = total.get((sem, q), 0) + len(es)
+        for (sem, q), n in total.items():
+            arrives((sem, q), sem + str(q), n)
+
+    def whole(part, q):
+        return [x for x in ((part, q), ("f" + part, q)) if x in wrote]
+
+    def send(call, buf):
+        trs, r = [], []
+        for d, q, part, c0, c1, es, sem in call:
             rid, pid = topo.addr(cores[d], core)
-            trs.append(RemoteDMATransfer(dst_ids=[DstId(rid=rid, pnc=pid)], dma_engine_mask=bits(lane(rank, d)),
-                                         remote_sem=T.sem[sem], src=src, dst=dst))
-            tot += len(lane(rank, d))
-        op("g", lambda: g.remote_dma_fused(trs, local_sem=T.sem.sent), r, (), remote=tot)
+            side = T[buf + str(q)][:, c0:c1]
+            trs.append(RemoteDMATransfer(dst_ids=[DstId(rid=rid, pnc=pid)], dma_engine_mask=bits(es), remote_sem=T.sem[sem + str(q)],
+                                         src=side, dst=side))
+            r += [("f" + part, q)] if ("f" + part, q) in wrote and q != rank else whole(part, q)
+        op("g", lambda: g.remote_dma_fused(trs, local_sem=T.sem.sent), r, (), remote=sum(len(x[5]) for x in call))
 
     def verdict_lane(a, d):
         off, on = lanes(a)
@@ -178,17 +233,10 @@ def rank_program(g, core, T, topo):
         h = len(off) // len(far)
         return on[:h] if near(a, d) else off[far.index(d) * h:(far.index(d) + 1) * h]
 
-    direct = [d for d in range(N) if d != rank and source_of(rank, d) == rank]
-    passes = [(q, d) for j in range(1, N) for q in [(rank + j) % N] for d in range(N)
-              if d not in (rank, q) and source_of(q, d) == rank]
-    for q in range(N):
-        if q != rank:
-            a = source_of(q, rank)
-            n = len(lane(a, rank))
-            for part in ("slab", "spow", "kap"):
-                arrives((part, q), (part if a == q else "slab") + str(q), n)
-            arrives(("sl", q, 0), "sl%d" % q, n)
-            arrives(("sl", q, 1), "sl%d" % q, n)
+    tables = [("slab", 0, NV), ("spow", NV, NV + NE), ("kap", NV + NE, NV + 2 * NE)]
+    mended = [("sl", 0, NV)]
+    expect(tables)
+    expect(mended)
     arrives("TL", "tm", sum(len(verdict_lane(a, rank)) for a in range(N) if a != rank))
 
     TAB = T["TAB%d" % rank]
@@ -196,14 +244,14 @@ def rank_program(g, core, T, topo):
     def load(q, out, in_, w):
         op(q, lambda: eng[q].dma_start(out, in_), (), [w], dma=True)
 
-    load("y", T.PX[:], T.px[:], "PX")
-    load("s", T.PY[:], T.py[:], "PY")
-    load("y", T.COR[:], T.cor[:], "COR")
+    load("s", T.PX[:], T.px[:], "PX")
+    load("y", T.PY[:], T.py[:], "PY")
     load("s", T.EN[:], T.en[:], "EN")
-    load("y", TAB[:, 0:NV], T.slab[:], ("slab", rank))
+    load("y", T.VX[:], T.vx[:], "VX")
     load("s", T.VY[:], T.vy[:], "VY")
-    load("s", T.VX[:], T.vx[:], "VX")
-    load("y", TAB[:, NV:NV + NE], T.spow[:], ("spow", rank))
+    load("y", TAB[:, 0:NV], T.slab[:], ("slab", rank))
+    load("s", T.COR[:], T.cor[:], "COR")
+    load("s", TAB[:, NV:NV + NE], T.spow[:], ("spow", rank))
     load("y", TAB[:, NV + NE:], T.kap[:], ("kap", rank))
     load("y", T.FM[:], T.fm[:], "FM")
 
@@ -214,166 +262,305 @@ def rank_program(g, core, T, topo):
     op("g", lambda: g.iota(T.PCI[:], [[0, 4]], 0, 1), (), ["PCI"])
     op("g", lambda: g.iota(T.IOI[:], [[1, 144]], 0, 0), (), ["IOI"])
     positions(0, 0, IOT0)
-    for part, c0, c1 in (("slab", 0, NV), ("spow", NV, NV + NE), ("kap", NV + NE, NV + 2 * NE)):
-        send(direct, TAB[:, c0:c1], TAB[:, c0:c1], part + str(rank), [(part, rank)])
-    positions(1, IOT0, 128)
-    for q, d in passes:
-        send([d], T["TAB%d" % q][:], T["TAB%d" % q][:], "slab%d" % q, [("slab", q), ("spow", q), ("kap", q)])
+    for k, call in enumerate(calls_of(rank, tables)):
+        send(call, "TAB")
+        if k == 1:
+            positions(1, IOT0, 128)
 
-    op("v", lambda: g.vector.memset(T.ZB[:], 0.0), (), ["ZB"])
-    ts(T.PCI[:, 1:2], T.PCI[:, 0:1], 112, Op.bitwise_and, r=["PCI"], w=["PC1"])
-    ts(T.PCI[:, 2:3], T.PCI[:, 0:1], 15, Op.bitwise_and, r=["PCI"], w=["PC2"])
-    cp(T.PCF[:], T.PCI[:], ["PCI", "PC1", "PC2"], ["PCF"])
-    pk, pg, pr = T.PCF[:, 0:1], T.PCF[:, 1:2], T.PCF[:, 2:3]
-    ts(T.I1[:], T.IOI[:, 0:128], 112, Op.bitwise_and, r=["IOI"], w=["I1"])
-    ts(T.SEL[:], T.IOI[:, 0:16], pr, Op.is_equal, r=["IOI", "PCF"], w=["SEL"])
-    ts(T.BD[:], T.I1[:], pg, Op.is_equal, r=["I1", "PCF"], w=["BD"])
-    ts(T.W[:], T.IOI[:], 15.0, Op.subtract, pg, Op.is_equal, r=["IOI", "PCF"], w=["W"])
-    ts(T.IDB[:], T.IOI[:, 0:128], pk, Op.is_equal, r=["IOI", "PCF"], w=["IDB"])
+    ck = ((128.0, 135.0), (-8.0, 0.0))
+    for k in range(2):
+        fill(T.CK[0:2, 128 * k:128 * k + 128], ck[k][1], [("CK", k)])
+    fill(T.ZB[:], 0.0, ["ZB"])
+    for k, x in ((1, 112), (2, 15), (3, 8)):
+        ts(T.PCI[:, k:k + 1], T.PCI[:, 0:1], x, Op.bitwise_and, r=["PCI"], w=[("PC", k)])
+    fill(T.ONE[:], 1.0, ["ONE"])
+    cp(T.PCF[:, 0:4], T.PCI[:], ["PCI"] + [("PC", k) for k in (1, 2, 3)], ["PCF"])
+    fill(T.D0[:], 0.0, ["D0"])
+    for k in range(2):
+        fill(T.CK[0:1, 128 * k:128 * k + 128], ck[k][0], [("CK", k)])
+
+    def const(out, k, n, start):
+        return (out, T.CK[0:2, 128 * k:128 * k + 128], T.ONE[0:2, 0:n], start, False)
+
+    pk, pg, pr, pf = [T.PCF[:, k:k + 1] for k in range(4)]
+    col = {}
+
+    def column(name, x, y):
+        k = 5 + len(col)
+        col[name] = T.PCF[:, k:k + 1]
+        ts(col[name], pf, (y - x) / 8, Op.mult, x, Op.add, r=["PCF"], w=[name])
+
+    tk = T.PCF[:, 4:5]
+    ts(tk, pk, pf, Op.subtract, 8.0, Op.add, r=["PCF"], w=["tk"])
+    column("v0", 1.0, 0.0)
+    column("v1", 0.0, 1.0)
+    column("vh", 1 / 16, 4.0)
+    column("vr", -4.0, -128.0)
+    column("rs", 1 / 64, 1 / 32)
+    column("ro", OR - (OH + 504) / 64, OR - (OH + 248) / 32)
+    column("wr", -64.0, -32.0)
+    column("cs", 1 / (4 * ALPHA), 0.0)
+    ts(T.F1[:], T.IOI[:], pg, Op.subtract, 11.0, Op.subtract, r=["IOI", "PCF"], w=["F1"])
     ts(T.IDF[:], T.IOI[:, 0:128], pk, Op.is_equal, r=["IOI", "PCF"], w=["IDF"])
-    ts(T.I2[:], T.IOI[:, 0:128], 15, Op.bitwise_and, r=["IOI"], w=["I2"])
-    ts(T.F1[:], T.IDF[:], 2.0, Op.mult, r=["IDF"], w=["F1"])
-    ts(T.H1[:], T.I2[:], pr, Op.is_equal, r=["I2", "PCF"], w=["H1"])
-    tt(T.M2[:], T.H1[:], T.F1[:], Op.add, ["H1", "F1"], ["M2"])
-    for k in LB:
-        mm([(PS[k][:], T.ZB[:, 0:128], T.ZB[:], True, False)], ["ZB"], [k])
+    ts(T.SEL[:], T.IOI[:, 0:16], pr, Op.is_equal, r=["IOI", "PCF"], w=["SEL"])
+    ts(T.I2[:], T.IOI[:, 0:128], 112, Op.bitwise_and, r=["IOI"], w=["I2"])
+    act(T.YL[:, 0:144], T.F1[:], Fn.Abs, ["F1"], ["F2"])
+    ts(T.S0[:], T.IOI[:, 0:136], tk, Op.is_equal, col["v0"], Op.mult, r=["IOI", "tk", "v0"], w=["S0"])
+    ts(T.BD[:], T.I2[:], pg, Op.is_equal, r=["I2", "PCF"], w=["BD"])
+    for name, x in (("IDB", 1.0), ("I8", 8.0)):
+        act(T[name][:], T.IDF[:], Fn.Copy, ["IDF"], [name], scale=x)
+    act(T.QQ[:, 0:128], T.IDF[:], Fn.Copy, ["IDF"], [("QQ", 0)], scale=128.0)
     for k in range(16):
         act(T.BR[:, 128 * k:128 * k + 128], T.BD[:], Fn.Copy, ["BD", "SEL"], [("BR", k)], scale=T.SEL[:, k:k + 1])
 
-    def cols(hs, o=0):
-        return slice(o + 32 * hs[0], o + 32 * hs[-1] + 32)
+    def vl(t, h, c0=0, c1=32):
+        o = 128 * t + 32 + 32 * h
+        return T.IL[:, o + c0:o + c1]
 
-    def toks(name, hs):
-        return [(name, h) for h in hs]
+    def el(t, h):
+        o = 128 * t + 96 * h
+        return T.IL[:, o:o + 32]
 
-    def fields(hs):
-        c = cols(hs)
-        ts(T.XH[:, c], T.Z[:, c], 4, Op.arith_shift_right, 63, Op.bitwise_and, r=toks("Z", hs), w=toks("XH", hs))
-        ts(T.YH[:, c], T.Z[:, c], YS - 2, Op.arith_shift_right, 31 << 6, Op.bitwise_and, r=toks("Z", hs), w=toks("YH", hs))
+    ts(T.I1[:], T.PY[:], 4, Op.arith_shift_right, r=["PY"], w=["I1"])
+    ts(T.I2[:], T.PX[:], 4, Op.arith_shift_right, r=["PX"], w=["I2"])
+    ts(T.S1[:], T.IOI[:, 0:136], tk, Op.is_equal, col["v1"], Op.mult, r=["IOI", "tk", "v1"], w=["S1"])
+    ts(T.I3[:], T.I1[:], 64.0, Op.mult, r=["I1"], w=["I3"])
+    ts(T.WY[:], T.YL[:, 0:136], 4.0, Op.is_equal, -ALPHA, Op.mult, r=["F2"], w=["WY"])
+    cp(T.PH[:, 0:128], T.PX[:], ["PX"], [("PH", 0)])
+    tt(T.I1[:], T.I3[:], T.I2[:], Op.add, ["I3", "I2"], ["I1"])
+    for h in range(2):
+        ts(el(0, h), T.EN[:, 32 * h:32 * h + 32], 1 / 64, Op.mult, -31.5 / 64, Op.add, r=["EN"], w=[("EL", 0, h)])
+    cp(T.PH[:, 128:256], T.PY[:], ["PY"], [("PH", 1)])
+    cp(vl(0, 0, 0, 64), T.I1[:, 0:64], ["I1"], [("VL", 0, 0), ("VL", 0, 1)])
+    ts(T.IDH[:], T.IOI[:, 0:128], pk, Op.is_equal, r=["IOI", "PCF"], w=["IDH"])
+    ts(T.I254[:], T.IOI[:, 0:128], pk, Op.is_equal, -254.0, Op.mult, r=["IOI", "PCF"], w=["I254"])
+    ts(T.D0[:, 2::3], T.ZB[:, 0:128], col["rs"], Op.add, r=["ZB", "rs", "D0"], w=["D02"])
+    for h in range(2):
+        ts(T.D1[:, 384 * h + 2:384 * h + 192:3], T.ZB[:, 0:64], col["ro"], Op.add, r=["ZB", "ro"], w=[("D12", h)])
+        ts(T.CQ[:, 192 * h:192 * h + 64], T.ZB[:, 0:64], col["wr"], Op.add, -float(OR), Op.mult, r=["ZB", "wr"], w=[("CQ", h, 0)])
+        fill(T.CQ[:, 64 + 96 * h:96 + 96 * h], -1800 / 64, [("CQ", h, 1)])
+    fill(T.CQ[:, 96:160], 132.0 * OR - 65 * OH // 16, [("CQ", 2)])
+    ts(T.GH[:], T.IOI[:, 0:136], tk, Op.is_equal, col["vh"], Op.mult, r=["IOI", "tk", "vh"], w=["GH"])
+    ts(T.GR[:], T.IOI[:, 0:136], tk, Op.is_equal, col["vr"], Op.mult, r=["IOI", "tk", "vr"], w=["GR"])
+    ts(T.DR[:], T.IOI[:, 0:128], pk, Op.is_equal, col["wr"], Op.mult, r=["IOI", "PCF", "wr"], w=["DR"])
+    fill(T.XS[:, 64:128], 0.0, ["XC"])
 
-    def voxel(hs):
-        c = cols(hs)
-        tt(T.V[:, c], T.XH[:, c], T.YH[:, c], Op.add, toks("XH", hs) + toks("YH", hs), toks("V", hs))
+    def regroup(u, z):
+        return [(ps(AB[z], 128 * u, 128 * u + 128), (T.S0, T.S1)[u][:, 8 - 8 * f:136 - 8 * f],
+                 T.PH[:, 256 * z + 128 * f:256 * z + 128 * f + 128], f == 0, f == 1 and z == 1) for f in range(2)]
 
-    def listed(par, hs):
-        cp(T.VI[:, cols(hs, 64 * par)], T.V[:, cols(hs)], toks("V", hs), [("VI", par, h) for h in hs])
+    def state():
+        cp(T.PH[:, 256:384], T.VX[:], ["VX"], [("PH", 2)])
+        cp(T.PH[:, 384:512], T.VY[:], ["VY"], [("PH", 3)])
+        mm(regroup(0, 1) + regroup(1, 1), ["S0", "S1", ("PH", 2), ("PH", 3)], [AB[1]])
+        ts(T.I2[:], T.COR[:], 15, Op.bitwise_and, r=["COR"], w=["I2"])
+        ts(T.I3[:], T.COR[:], 4, Op.arith_shift_right, r=["COR"], w=["I3"])
+        ts(T.F2[:], T.I2[:], 128.0, Op.mult, r=["I2"], w=["F3"])
+        for u in range(2):
+            cp(T.DH[:, u::2], ps(AB[1], 128 * u, 128 * u + 128), w=[("DH", u)], b=[AB[1]])
+        for u in range(2):
+            mm(regroup(u, 0) + [(ps(AB[0], 128 * u, 128 * u + 128), T.I254[:], T.DH[:, u::2], False, True)],
+               ["S0", "S1", "I254", ("PH", 0), ("PH", 1), ("DH", u)], [AB[0]])
+        tt(T.I2[:], T.F2[:], T.I3[:], Op.add, ["F3", "I3"], ["I2"])
+        begin(0)
+        cp(T.PU[:], T.I2[:], ["I2"], ["PU"])
+        for u in range(2):
+            ts(T.X0[:, u::2], ps(AB[0], 128 * u, 128 * u + 128), OH - 7.5, Op.add, w=[("X0", u)], b=[AB[0]])
+        places(0)
+        strides(0)
 
-    def record(par, hs, src, tok):
-        ts(T.EI[:, cols(hs, 64 * par)], src, 1.0 / 64, Op.mult, -31.5 / 64, Op.add, r=[tok], w=[("EI", par, h) for h in hs])
+    def uc(h):
+        return ps(QB[h], 64, 96) if h == 0 else ps(QB[h], 32, 64)
 
-    def wrap(hs):
-        ts(T.ZW[:, cols(hs)], T.Z[:, cols(hs)], (511 << YS) | 1023, Op.bitwise_and, r=toks("Z", hs), w=toks("ZW", hs))
+    def vc(h):
+        return ps(QB[h], 96, 128) if h == 0 else ps(QB[h], 0, 32)
+
+    def wc(h):
+        return ps(QB[h], 64 * h, 64 * h + 64)
+
+    def yc(h):
+        return ps(PB[h], 0, 64)
+
+    def dc(h):
+        return ps(PB[h], 64, 128)
+
+    def kept(h):
+        return T.D1[:, 288 * h + 1:288 * h + 288:3]
 
     def begin(b):
-        c, hs = slice(64 * b, 64 * b + 64), [0, 1]
-        ts(T.MD[:], T.PY[:, c], float(1 << YS), Op.mult, r=["PY"], w=["MD"])
-        record(0, hs, T.EN[:, c], "EN")
-        tt(T.Z[:], T.MD[:], T.PX[:, c], Op.add, ["MD", "PX"], toks("Z", hs))
-        fields(hs)
-        wrap(hs)
-        voxel(hs)
-        listed(0, hs)
+        dh = [("DH", u) for u in range(2)]
+        ts(T.D1[:, 193:384:3], T.EN[:, 64 * b:64 * b + 64], 1 / 64, Op.mult, r=["EN"], w=[("US", 0), ("US", 1)])
+        for h in range(2):
+            c = 128 * b + 64 * h
+            cp(T.D1[:, 384 * h:384 * h + 192:3], T.DH[:, c:c + 64], dh, [("D10", h)])
 
-    begin(0)
-    ts(T.I1[:], T.COR[:], 15, Op.bitwise_and, r=["COR"], w=["I1"])
-    ts(T.I3[:], T.COR[:], 4, Op.arith_shift_right, r=["COR"], w=["I3"])
-    ts(T.F1[:], T.I1[:], 128.0, Op.mult, r=["I1"], w=["F1"])
-    cp(T.CU[:], T.COR[:], ["COR"], ["CU"])
-    tt(T.I2[:], T.F1[:], T.I3[:], Op.add, ["F1", "I3"], ["I2"])
-    cp(T.PU[:], T.I2[:], ["I2"], ["PU"])
-    ts(T.I1[:], T.VY[:], 256.0, Op.add, r=["VY"], w=["I1"])
-    ts(T.F2[:], T.VX[:], 2.0, Op.mult, r=["VX"], w=["F2"])
-    ts(T.I2[:], T.I1[:], 511, Op.bitwise_and, r=["I1"], w=["I2"])
-    ts(T.F1[:], T.I2[:], -256.0, Op.add, float(2 << YS), Op.mult, r=["I2"], w=["F1"])
-    tt(T.D2[:], T.F1[:], T.F2[:], Op.add, ["F1", "F2"], ["D2"])
+    def places(b):
+        for h in range(2):
+            c = 128 * b + 64 * h
+            cp(T.D1[:, 384 * h + 1:384 * h + 192:3], T.X0[:, c:c + 64], [("X0", 0), ("X0", 1)], [("XD", h)])
+
+    def strides(b):
+        for h in range(2):
+            c = 128 * b + 64 * h
+            mm([(dc(h), T.IDH[:], T.DH[:, c:c + 64], True, True)], ["IDH", ("DH", 0), ("DH", 1)], [PB[h]])
+
+    def seed(b, h):
+        o = 128 * b + 64 * h
+        mm([(ps(QB[h], 0, 128), T.IDB[:], T.CQ[:, 128 * h:128 * h + 128], True, False),
+            (ps(QB[h], 32 * h, 32 * h + 96), T.IDF[:], kept(h), False, False), (wc(h), T.I254[:], T.DH[:, o:o + 64], False, False)],
+           ["IDB", "IDF", "I254", ("CQ", h, 0), ("CQ", h, 1), ("CQ", 2), ("XD", h), ("US", h)], [QB[h]])
+
+    for k in LB:
+        mm([(ps(k), T.ZB[:, 0:128], T.ZB[:], True, False)], ["ZB"], [k])
+
+    spare = [
+        lambda: cp(T.CU[:], T.COR[:], ["COR"], ["CU"]),
+        lambda: ts(T.I3[:], T.IOI[:, 0:128], 15, Op.bitwise_and, r=["IOI"], w=["I3"]),
+        lambda: cp(vl(NS, 0, 0, 64), T.I1[:, 64:128], ["I1"], [("VL", NS, 0), ("VL", NS, 1)]),
+        lambda: ts(T.H1[:], T.I3[:], pr, Op.is_equal, 64.0, Op.mult, r=["I3", "PCF"], w=["H1"]),
+        lambda: ts(T.NF[:], T.FM[:], -1 / 64, Op.mult, r=["FM"], w=["NF"]),
+        lambda: tt(T.M2[:], T.H1[:], T.QQ[:, 0:128], Op.add, ["H1", ("QQ", 0)], ["M2"]),
+        lambda: ts(T.WL[:], T.F1[:], 4.0, Op.is_equal, -1 / 64, Op.mult, r=["F1"], w=["WL"]),
+    ] + [lambda h=h: ts(el(NS, h), T.EN[:, 64 + 32 * h:96 + 32 * h], 1 / 64, Op.mult, -31.5 / 64, Op.add, r=["EN"],
+                        w=[("EL", NS, h)]) for h in range(2)]
 
     def table(t):
         return (rank + (t % NS) // S) % N
 
-    def lmul(t, h, u):
-        par, q, x = t % 2, table(t), 4 * h + u
-        o = 1024 * par + 128 * x
-        if u < BY_SCALAR[t]:
-            k = AB[2 * par + h]
-            tt(T.AK[:, o:o + 128], PS[k][:, 128 * u:128 * u + 128], T.K[:, o:o + 128], Op.mult, [("K", par, h)], [("AK", par, x)], [k])
-        else:
-            win = T["TAB%d" % q][:, NV + NE:].indirect(T.EI[:, 64 * par + 8 * x:64 * par + 8 * x + 8])
-            tt(T.AK[:, o:o + 128], win, T.A[:, o:o + 128], Op.mult, [("kap", q), ("EI", par, h), ("A", par, x)], [("AK", par, x)])
-
-    def acopy(t, h):
-        par, n = t % 2, 128 * BY_SCALAR[t]
-        if n > 0:
-            k, o = AB[2 * par + h], 1024 * par + 512 * h
-            mm([(PS[k][:, 0:n], T.IDB[:], T.A[:, o:o + n], True, True)], ["IDB"] + [("A", par, 4 * h + x) for x in range(4)], [k])
-
-    def energies(b, t):
-        n = 1 - t % 2
-        ts(T.E1[:], T.U[:, 64 * n:64 * n + 64], 0.0, Op.max, r=[("U", n, 0), ("U", n, 1)], w=["E1"])
-        ts(T.E2[:], T.E1[:], 1023, Op.bitwise_and, r=["E1"], w=["E2"])
-        cp(T.YE[:, 64 * b:64 * b + 64], T.E2[:], ["E2"], [("YE", b)])
-
-    def step(t):
-        if t % NS == 0:
-            gather(t, 0)
-            gather(t, 1)
-            for c in range(4):
-                prod(t, 0, c)
-            losses(t, 0)
-            after(t, 0)
-        if t == NS:
-            acopy(t - 1, 0)
-            acopy(t - 1, 1)
-            later.extend((t - 1, h) for h in range(2))
-        phase(t, 0, (t, 1))
-        if t == NS - 1:
-            phase(t, 1, None)
-            mend(t)
-        elif t == B * NS - 1:
-            phase(t, 1, None)
-            energies(1, t)
-            op("y", lambda: g.sync.dma_start(T.ye[:], T.YE[:]), [("YE", 0), ("YE", 1)], (), dma=True)
-        else:
-            phase(t, 1, (t + 1, 0))
-
-    later = []
+    cut = [sum(GA[:i]) for i in range(len(GA) + 1)]
 
     def gather(t, h):
-        par, q = t % 2, table(t)
+        q = table(t)
         win = T["TAB%d" % q][:, 0:NV] if t < NS else T["SL%d" % q][:]
-        wtok = [("slab", q)] if t < NS else [("sl", q, 0), ("sl", q, 1)]
-        for u in range(4 * h, 4 * h + 4, AW):
-            o = 1024 * par + 128 * u
-            act(T.A[:, o:o + 128 * AW], win.indirect(T.VI[:, 64 * par + 8 * u:64 * par + 8 * (u + AW)]), Fn.Copy,
-                wtok + [("VI", par, h)], [("A", par, u + x) for x in range(AW)])
+        wtok = whole("slab" if t < NS else "sl", q)
+        for u in range(len(GA)):
+            o = P * t + 512 * h
+            act(T.A[:, o + cut[u]:o + cut[u + 1]], win.indirect(vl(t, h, cut[u] // 16, cut[u + 1] // 16)), Fn.Copy,
+                wtok + [("VL", t, h)], [("A", t, h, u)])
 
-    def prod(t, h, c):
-        par, q, u = t % 2, table(t), 4 * h + c
-        if WIDE > 1:
-            if c % WIDE:
-                return
-        sw = T["TAB%d" % q][:, NV:NV + NE].indirect(T.EI[:, 64 * par + 8 * u:64 * par + 8 * (u + WIDE)])
-        o = 1024 * par + 128 * u
-        tt(T.PR[:, 128 * u:128 * (u + WIDE)], sw, T.A[:, o:o + 128 * WIDE], Op.mult,
-           [("spow", q), ("EI", par, h)] + [("A", par, u + i) for i in range(WIDE)], [("PR", u + i) for i in range(WIDE)])
+    def prod(t, h, u):
+        q, o = table(t), 128 * t + 96 * h
+        sw = T["TAB%d" % q][:, NV:NV + NE].indirect(T.IL[:, o + cut[u] // 16:o + cut[u + 1] // 16])
+        o = P * t + 512 * h
+        tt(T.PR[:, 512 * h + cut[u]:512 * h + cut[u + 1]], sw, T.A[:, o + cut[u]:o + cut[u + 1]], Op.mult,
+           whole("spow", q) + [("EL", t, h), ("A", t, h, u)], [("PR", h, u)])
 
     def losses(t, h):
-        k = (PA, PB)[h]
-        mm([(PS[k][:, 0:32], T.W[:, 15 - r:143 - r], T.PR[:, 512 * h + r:512 * h + 512:16], r == 0, r == 15) for r in range(16)],
-           ["W"] + [("PR", 4 * h + c) for c in range(4)], [k])
+        pr_ = [("PR", h, u) for u in range(len(GA))]
+        if t % NS == NS - 1:
+            mm([(uc(h), T.WL[:, 15 - r:143 - r], T.PR[:, 512 * h + r:512 * h + 512:16], False, r == 15) for r in range(16)],
+               ["WL"] + pr_, [QB[h]])
+        else:
+            mm([const(yc(h), 0, 64, True)]
+               + [(yc(h), T.WY[:, 7 - r:135 - r], T.PR[:, 512 * h + r:512 * h + 512:8], False, r == 7) for r in range(8)],
+               ["WY", "ONE", ("CK", 0)] + pr_, [PB[h]])
+
+    done = {"A": 0, "k": 0, "a": 0, "L": 0, "add": 0, "copied": 0}
+    NL = 512 // LW
+
+    def coefficients():
+        n = done["k"]
+        if n >= done["A"] or 2 * n > done["add"] + 2 * KR - 2:
+            return
+        t, h, q = n // 2, n % 2, table(n // 2)
+        if n not in FUSED:
+            act(T.K[:, 512 * (n % KR):512 * (n % KR) + 512], T["TAB%d" % q][:, NV + NE:].indirect(el(t, h)), Fn.Copy,
+                whole("kap", q) + [("EL", t, h)], [("K", n % KR)])
+        done["k"] += 1
+
+    def acopy():
+        n, u = done["a"] // 2, done["a"] % 2
+        if n >= done["k"] or NL * (n - 1) > done["L"]:
+            return
+        k = AB[n % 2]
+        if n in FUSED or (n in BY_DMA and u == 0):
+            pass
+        elif u == 0:
+            mm([const(ps(k), 1, 512, True)], ["ONE", ("CK", 1)], [k])
+        else:
+            mm([(ps(k), T.IDB[:], T.A[:, 512 * n:512 * n + 512], n in BY_DMA, True)],
+               ["IDB"] + [("A", n // 2, n % 2, x) for x in range(len(GA))], [k])
+        done["a"] += 1
+
+    def lmul():
+        n, u = done["L"] // NL, done["L"] % NL
+        if 2 * n + 2 > done["copied"] or 2 * n > done["add"] + 2:
+            if spare:
+                spare.pop(0)()
+            return
+        o = 512 * (n % 4) + LW * u
+        out, tok = T.AK[:, o:o + LW], ("AK", n % 4, u)
+        if n in BY_DMA:
+            x = BY_DMA.index(n) % RING
+            while len(pending) >= RING:
+                summed()
+            out, tok = T.AD[:, 512 * x + LW * u:512 * x + LW * u + LW], ("AD", x, u)
+        if n in FUSED:
+            t, h, q = n // 2, n % 2, table(n // 2)
+            c = 128 * t + 96 * h + LW * u // 16
+            tt(out, T["TAB%d" % q][:, NV + NE:].indirect(T.IL[:, c:c + LW // 16]), T.A[:, 512 * n + LW * u:512 * n + LW * u + LW],
+               Op.mult, whole("kap", q) + [("EL", t, h)] + [("A", t, h, x) for x in range(len(GA))], [tok])
+        else:
+            o = 512 * (n % KR) + LW * u
+            tt(out, ps(AB[n % 2], LW * u, LW * u + LW), T.K[:, o:o + LW], Op.mult, [("K", n % KR)], [tok], [AB[n % 2]])
+        done["L"] += 1
+
+    def ladd():
+        n, u = done["add"] // 2, done["add"] % 2
+        if NL * (n + u) > done["L"] or n >= done["k"]:
+            return
+        h, o, last = n % 2, 512 * (n % 4), n // 2 == B * NS - 1 and u == 1
+        if n in BY_DMA:
+            if u == 1:
+                pending.append(n)
+        elif u == 0:
+            mm([(ps(LB[h]), T.I8[:], T.K[:, 512 * (n % KR):512 * (n % KR) + 512], False, False)], ["I8", ("K", n % KR)], [LB[h]])
+        else:
+            mm([(ps(LB[h]), T.IDH[:], T.AK[:, o:o + 512], False, last)], ["IDH"] + [("AK", n % 4, x) for x in range(NL)], [LB[h]])
+        done["add"] += 1
+        if n // 2 in JOIN:
+            assert not pending
+            x = NACC * h + JOIN.index(n // 2)
+            mm([(ps(LB[h], 256 * u, 256 * u + 256), T.IDF[:], T.LD[:, 512 * x + 256 * u:512 * x + 256 * u + 256], False, False)],
+               ["IDF", ("LD", x)], [LB[h]])
+        if last:
+            act(T.YL[:, 512 * h:512 * h + 512], ps(LB[h]), Fn.Exp, (), [("YL", h), "F2"], [LB[h]], scale=-1.0 / 128)
+            op("y", lambda: g.sync.dma_start(T.yl[:, 512 * h:512 * h + 512], T.YL[:, 512 * h:512 * h + 512]), [("YL", h)], (), dma=True)
+
+    pending, turn = [], [0, 0]
+
+    def summed():
+        if pending:
+            n = pending.pop(0)
+            x, y = NACC * (n % 2) + turn[n % 2] % NACC, BY_DMA.index(n) % RING
+            turn[n % 2] += 1
+            kw = {"accum_op": Op.add} if ("LD", x) in wrote else {}
+            op("g", lambda: g.dma_start(T.LD[:, 512 * x:512 * x + 512], T.AD[:, 512 * y:512 * y + 512], **kw),
+               [("AD", y, z) for z in range(NL)], [("LD", x)], dma=True)
+
+    def lrun(items):
+        end = max(min(done["add"] // 2 + items, done["A"]), (done["a"] + 1) // 2)
+        while done["add"] < 2 * end:
+            coefficients()
+            done["copied"] = done["a"]
+            for _ in range(2):
+                if done["a"] < 2 * end:
+                    acopy()
+            for _ in range(2):
+                for _ in range(NL // 2):
+                    lmul()
+                ladd()
 
     def after(t, h):
-        par, q, ph = t % 2, table(t), 2 * t + h
-        if t != NS - 1:
-            acopy(t, h)
+        ph = 2 * t + h
+        done["A"] = ph + 1
+        for _ in range(KPLAN[ph]):
+            coefficients()
         if t < NS and REORDER[ph]:
             c0 = sum(REORDER[:ph])
             c1 = c0 + REORDER[ph]
             act(T.AC[:, 16 * c0:16 * c1], TAB[:, 0:NV].indirect(T.CU[:, c0:c1]), Fn.Identity,
-                [("slab", rank), "CU"], ["AC"], bias=-15.0)
-        if BY_SCALAR[t]:
-            n, o, c = 128 * BY_SCALAR[t], 1024 * par + 512 * h, 64 * par + 32 * h
-            act(T.K[:, o:o + n], T["TAB%d" % q][:, NV + NE:].indirect(T.EI[:, c:c + n // 16]), Fn.Copy,
-                [("kap", q), ("EI", par, h)], [("K", par, h)])
+                [("slab", rank), "CU"], [("AC", ph)], bias=-15.0)
         if t < NS and SCATTER[ph]:
             c0 = sum(SCATTER[:ph])
             c1 = c0 + SCATTER[ph]
@@ -381,94 +568,125 @@ def rank_program(g, core, T, topo):
                 ["PU", ("IOT", 0)] + ([("IOT", 1)] if c1 > IOT0 else []), ["INVW"])
             if c1 == 128:
                 op("y", lambda: g.sync.dma_start(T.INVL[:], T.INVW[0::16, :]), ["INVW"], ["INVL"], dma=True)
-        if t != NS - 1:
-            later.append((t, h))
 
     def phase(t, h, other):
-        b, i, par, k = t // NS, t % NS, t % 2, (PA, PB)[h]
-        end = t == B * NS - 1
-        c = slice(32 * h, 32 * h + 32)
-        d, m, md = PS[k][:, 0:32], PS[k][:, 64:96], PS[k][:, 128:160]
-        o, n = 64 * par + 32 * h, 64 * (1 - par) + 32 * h
-        usrc, utok = (T.EN[:, 64 * b + 32 * h:64 * b + 32 * h + 32], "EN") if i == 0 else (T.U[:, o:o + 32], ("U", par, h))
-        unew, ntok = T.U[:, n:n + 32], ("U", 1 - par, h)
-        todo = [later.pop(0) for _ in range(min(len(later), 2))]
-        pieces = [(x, u) for x in todo for u in range(4)]
+        b, i = t // NS, t % NS
+        c = slice(64 * h, 64 * h + 64)
+        c32 = slice(32 * h, 32 * h + 32)
+        mcol = T.D0[:, 192 * h + 1:192 * h + 192:3]
         if other and (i, h) != (0, 0):
             gather(*other)
+            after(*other)
+        nbig = [0]
+        done["copied"] = done["a"]
+        if (2 * i + h + PASS) % (2 * S) == 0:
+            for call in passes_of(rank, (tables, mended)[b], (2 * i + h + PASS) // (2 * S)):
+                send(call, ("TAB", "SL")[b])
+        for _ in range(SUMS[2 * t + h]):
+            summed()
 
-        def big(cc):
-            if other:
-                prod(other[0], other[1], cc)
-                if cc == 3:
-                    losses(*other)
-                    after(*other)
-
-        def part(num):
-            for _ in range(num * len(todo)):
-                if pieces:
-                    (tt_, hh), u = pieces.pop(0)
-                    lmul(tt_, hh, u)
-                    if u == 3:
-                        last = tt_ == B * NS - 1
-                        mm([(PS[LB[hh]][:], T.IDF[:], T.AK[:, 1024 * (tt_ % 2) + 512 * hh:1024 * (tt_ % 2) + 512 * hh + 512], False, last)],
-                           ["IDF"] + [("AK", tt_ % 2, 4 * hh + x) for x in range(4)], [LB[hh]])
-                        if last:
-                            act(T.YL[:, 512 * hh:512 * hh + 512], PS[LB[hh]][:], Fn.Exp, (), [("YL", hh)], [LB[hh]], scale=-1.0 / 128)
-                            op("y", lambda: g.sync.dma_start(T.yl[:, 512 * hh:512 * hh + 512], T.YL[:, 512 * hh:512 * hh + 512]),
-                               [("YL", hh)], (), dma=True)
-
-        if end:
-            part(4)
-            for cc in range(4):
-                big(cc)
-            tt(unew, usrc, d, Op.subtract, [utok], [ntok], [k])
-        elif i == NS - 1:
-            tt(m, T.UF[:, c], d, Op.subtract, [("UF", h)], [("PM", h)], [k])
-            big(0)
-            tt(T.Z2[:, c], m, T.NF[:, c], Op.max, [("PM", h), "NF"], [("Z2", h)], [k])
-            tt(unew, usrc, d, Op.subtract, [utok], [ntok], [k])
-            big(1)
-            big(2)
-            ts(T.SG[:, c], T.Z2[:, c], -1.0, Op.max, 1.0, Op.min, r=[("Z2", h)], w=[("SG", h)])
-            big(3)
-            part(4)
-        else:
-            nbig = [0]
-
-            def products():
-                big(nbig[0])
+        def products():
+            if other and nbig[0] < len(GA):
+                prod(other[0], other[1], nbig[0])
                 nbig[0] += 1
+                if nbig[0] == len(GA):
+                    losses(*other)
 
+        def save():
+            tt(kept(h), ps(QB[h], 32 * h, 32 * h + 96), T.XS[:, 96 * h:96 * h + 96], Op.add,
+               [("XS", h), "XC"], [("XD", h), ("US", h)], [QB[h]])
+            if i == NS - 2:
+                seq = [(uc(h), T.IDF[:], T.D1[:, 193 + 96 * h:288 + 96 * h:3], True, False)]
+                if b == 0:
+                    seq += [(uc(h), T.IDF[:], T.NF[:, c32], False, False)]
+                mm(seq, ["IDF", "NF", ("US", h)], [QB[h]])
+
+        def scan():
+            op("v", lambda: g.vector.tensor_tensor_scan(T.SC[:, 192 * h + 192:192 * h + 384], T.D0[:, 192 * h:192 * h + 192],
+                                                        T.D1[:, 384 * h:384 * h + 192], 0.0, Op.mult, Op.add),
+               [("MM", h), "D02", ("D10", h), ("XD", h), ("D12", h)], [("SC", h)])
+
+        def voxels():
+            o, uv = 192 * h + 192, ps(QB[h], 64 - 64 * h, 128 - 64 * h)
+            seq = [(wc(h), T.DR[:], T.SC[:, o + 2:o + 192:3], False, False)]
+            seq += [(uv, T.GH[:, 8 - 8 * u:136 - 8 * u], T.SC[:, 384 * h + 1 + 3 * u:384 * h + 384:6], False, False) for u in range(2)]
+            seq += [(vc(h), T.GR[:, 8 - 8 * u:136 - 8 * u], T.SC[:, o + 2 + 3 * u:o + 192:6], False, u == 1) for u in range(2)]
+            mm(seq, ["GH", "GR", "DR", ("SC", h), ("CC", h)], [QB[h]])
+
+        def lists():
+            o = 128 * (t + 1) + 64 * h
+            ts(T.IL[:, o:o + 64], ps(QB[h], 64 - 64 * h, 128 - 64 * h), -31.5 / 64, Op.add,
+               w=[("VL", t + 1, h), ("EL", t + 1, h)], b=[QB[h]])
+
+        if t == B * NS - 1:
+            if h == 0:
+                lrun(2 * B * NS - 1 - done["add"] // 2)
+                acopy()
+                acopy()
+            for _ in GA:
+                products()
+            lrun(1)
+            ts(T.E1[:, c32], uc(h), 64.0, Op.mult, 0.0, Op.max, w=[("E1", h)], b=[QB[h]])
+        elif i == NS - 1:
+            tt(T.Z2[:, c32], uc(h), T.NF[:, c32], Op.max, ["NF"], [("Z2", h)], [QB[h]])
+            products()
+            ts(T.SG[:, c32], T.Z2[:, c32], -1 / 64, Op.max, 1 / 64, Op.min, r=[("Z2", h)], w=[("SG", h)])
+            for _ in GA:
+                products()
+        else:
             calls = {
-                "q": lambda: ts(T.Q[:, c], d, -0.005, Op.mult, 5.4975, Op.add, w=[("Q", h)], b=[k]),
-                "m": lambda: ts(m, T.Q[:, c], 0.5, Op.max, 2.0, Op.min, r=[("Q", h)], w=[("PM", h)], b=[k]),
-                "d": lambda: tt(md, m, T.D2[:, 64 * b + 32 * h:64 * b + 32 * h + 32], Op.mult, [("PM", h), "D2"], [("PD", h)], [k]),
-                "z": lambda: tt(T.Z[:, c], md, T.ZW[:, c], Op.add, [("PD", h), ("ZW", h)], [("Z", h)], [k]),
-                "f": lambda: fields([h]), "v": lambda: voxel([h]), "i": lambda: listed(1 - par, [h]),
-                "u": lambda: tt(unew, usrc, d, Op.subtract, [utok], [ntok], [k]),
-                "e": lambda: record(1 - par, [h], unew, ntok), "w": lambda: wrap([h]),
-                "P": products, "L": lambda: part(1),
+                "m": lambda: ts(mcol, yc(h), 255.0, Op.max, 258.0, Op.min, r=["D0"], w=[("MM", h)], b=[PB[h]]),
+                "c": lambda: ts(T.SC[:, 576 * h + 1:576 * h + 192:3], yc(h), 263 - 1800 * ALPHA, Op.subtract, col["cs"], Op.mult,
+                                r=["cs"], w=[("CC", h)], b=[PB[h]]),
+                "d": lambda: tt(T.XS[:, 128 * h:128 * h + 64], dc(h), mcol, Op.mult, [("MM", h)], [("XS", h)], [PB[h]]),
+                "z": scan, "W": lambda: seed(b, h), "s": save, "V": voxels, "i": lists, "P": products, "a": acopy, "L": lmul, "A": ladd,
             }
             for x in ORDER:
                 calls[x]()
-            if b == 0 and i % S == S - 2:
-                j = 128 * (i // S) + 32 * h
-                ts(T.KM[:, j:j + 32], T.V[:, c], float(P), Op.is_lt, r=[("V", h)], w=[("KM", i // S, 0, h)])
-                ts(T.KM[:, j + 64:j + 96], T.V[:, c], float(P), Op.is_ge, r=[("V", h)], w=[("KM", i // S, 1, h)])
-            if t == NS - 3 and h == 0:
-                ts(T.NF[:], T.FM[:], -1.0, Op.mult, r=["FM"], w=["NF"])
-            if t == NS - 2:
-                tt(T.UF[:, c], unew, T.NF[:, c], Op.add, [ntok, "NF"], [("UF", h)])
+            if b == 0 and i % S == S - 2 and h == 1:
+                j = 128 * (i // S)
+                vv = [("VL", t + 1, 0), ("VL", t + 1, 1)]
+                ts(T.KM[:, j:j + 64], vl(t + 1, 0, 0, 64), float(P), Op.is_lt, r=vv, w=[("KM", i // S, 0)])
+                ts(T.KM[:, j + 64:j + 128], vl(t + 1, 0, 0, 64), float(P), Op.is_ge, r=vv, w=[("KM", i // S, 1)])
+
+    def energies(b):
+        ts(T.E2[:], T.E1[:], 1023, Op.bitwise_and, r=[("E1", 0), ("E1", 1)], w=["E2"])
+        cp(T.YE[:, 64 * b:64 * b + 64], T.E2[:], ["E2"], [("YE", b)])
+
+    def step(t):
+        if t % NS == 0:
+            gather(t, 0)
+            gather(t, 1)
+            if t == 0:
+                state()
+            after(t, 0)
+            after(t, 1)
+            for u in range(len(GA)):
+                prod(t, 0, u)
+            losses(t, 0)
+            for _ in range(4):
+                acopy()
+        while t == S and spare:
+            spare.pop(0)()
+        phase(t, 0, (t, 1))
+        if t == NS - 1:
+            phase(t, 1, None)
+            mend(t)
+        elif t == B * NS - 1:
+            phase(t, 1, None)
+            energies(1)
+            op("y", lambda: g.sync.dma_start(T.ye[:], T.YE[:]), [("YE", 0), ("YE", 1)], (), dma=True)
+        else:
+            phase(t, 1, (t + 1, 0))
 
     def band(j):
-        return [("KM", j, x, h) for x in range(2) for h in range(2)]
+        return [("KM", j, x) for x in range(2)]
 
     def mend(t):
-        mm([(PS[PB][:, 64 * h:64 * h + 64], T.M2[:], T.SG[:], True, True) for h in range(2)], ["M2", ("SG", 0), ("SG", 1)], [PB])
+        pa, pb = PB
+        mm([(ps(pb, 64 * h, 64 * h + 64), T.M2[:], T.SG[:], True, True) for h in range(2)], ["M2", ("SG", 0), ("SG", 1)], [pb])
         for j in (1, 2, 3):
-            tt(T.TY[:, 128 * j:128 * j + 128], PS[PB][:, 0:128], T.KM[:, 128 * j:128 * j + 128], Op.mult,
-               band(j), [("TY", j)], [PB])
+            tt(T.TY[:, 128 * j:128 * j + 128], ps(pb, 0, 128), T.KM[:, 128 * j:128 * j + 128], Op.mult, band(j), [("TY", j)], [pb])
         ts(T.TO[:, 128:512], T.TY[:, 128:512], -1.0, Op.max, 1.0, Op.min, r=[("TY", j) for j in (1, 2, 3)], w=["TO"])
         trs, tot = [], 0
         for j in range(1, N):
@@ -478,66 +696,78 @@ def rank_program(g, core, T, topo):
                                          remote_sem=T.sem.tm, src=T.TO[:, 128 * j:128 * j + 128], dst=T.TL[:, 128 * j:128 * j + 128]))
             tot += len(verdict_lane(rank, dd))
         op("g", lambda: g.remote_dma_fused(trs, local_sem=T.sem.sent), ["TO"], (), remote=tot)
-        tt(T.TY[:, 0:128], PS[PB][:, 0:128], T.KM[:, 0:128], Op.mult, band(0), [("TY", 0)], [PB])
-        for c in (2, 3, 0, 1):
-            mm([(PS[AB[c]][:], T.ZB[:, 0:128], T.ZB[:], True, False)]
-               + [(PS[AB[c]][:, 128 * k:128 * k + 128], T.IDB[:], T.AC[:, 4 * c + k::16], False, False) for k in range(4)],
-               ["ZB", "IDB", "AC"], [AB[c]])
+        tt(T.TY[:, 0:128], ps(pb, 0, 128), T.KM[:, 0:128], Op.mult, band(0), [("TY", 0)], [pb])
+        tt(T.E0[:], T.Z2[:], T.NF[:], Op.subtract, [("Z2", 0), ("Z2", 1), "NF"], ["E0"])
         ts(T.TO[:, 0:128], T.TY[:, 0:128], -1.0, Op.max, 1.0, Op.min, r=[("TY", 0)], w=["T0"])
-        ts(T.INVU[:], T.INVL[:], 0.25 - IOFF, Op.add, r=["INVL"], w=["INVU"])
+        ts(T.E1[:], T.E0[:], 64.0, Op.mult, r=["E0"], w=[("E1", 0), ("E1", 1)])
         ts(T.MN[:, 0:128], T.TO[:, 0:128], 0.0, Op.min, r=["T0"], w=[("MN", 0)])
         begin(1)
-        energies(0, t)
+        energies(0)
+        places(1)
+        ac = [("AC", ph) for ph in range(2 * NS) if REORDER[ph]]
+        zb = (QB[0], QB[1], AB[0], AB[1])
+        for c in range(4):
+            if c == 2:
+                lrun(MENDL)
+            mm([(ps(zb[c]), T.ZB[:, 0:128], T.ZB[:], True, False)]
+               + [(ps(zb[c], 128 * k, 128 * k + 128), T.IDB[:], T.AC[:, 4 * c + k::16], False, False) for k in range(4)],
+               ["ZB", "IDB"] + ac, [zb[c]])
         tj = [T.TO[:, 0:128]] + [T.TL[:, 128 * j:128 * j + 128] for j in range(1, N)]
 
-        def total(k, col, js):
-            return [(PS[k][:, 128 * col:128 * col + 128], T.IDB[:], tj[j], n == 0, n == len(js) - 1) for n, j in enumerate(js)]
+        def total(k, cl, js):
+            return [(ps(k, 128 * cl, 128 * cl + 128), T.IDB[:], tj[j], n == 0, n == len(js) - 1) for n, j in enumerate(js)]
 
-        def least(name, n, k, col):
-            tt(T[name][:, 128 * n + 128:128 * n + 256], PS[k][:, 128 * col:128 * col + 128], T[name][:, 128 * n:128 * n + 128],
+        def least(name, n, k, cl):
+            tt(T[name][:, 128 * n + 128:128 * n + 256], ps(k, 128 * cl, 128 * cl + 128), T[name][:, 128 * n:128 * n + 128],
                Op.min, [(name, n)], [(name, n + 1)], [k])
 
-        mm(total(PA, 0, (0, 1)) + total(PA, 1, (0, 1, 2)), ["IDB", "T0", "TL"], [PA])
-        mm(total(PB, 0, (0, 1, 2, 3)) + total(PB, 1, (2, 3)), ["IDB", "T0", "TL"], [PB])
+        mm(total(pa, 0, (0, 1)) + total(pa, 1, (0, 1, 2)), ["IDB", "T0", "TL"], [pa])
+        mm(total(pb, 0, (0, 1, 2, 3)) + total(pb, 1, (2, 3)), ["IDB", "T0", "TL"], [pb])
         ts(T.HM[:, 0:128], tj[3], 0.0, Op.min, r=["TL"], w=[("HM", 0)])
-        least("MN", 0, PA, 0)
-        least("MN", 1, PA, 1)
-        mm(total(PA, 2, (1, 2, 3)), ["IDB", "TL"], [PA])
-        least("HM", 0, PB, 1)
-        least("MN", 2, PB, 0)
-        least("HM", 1, PB, 0)
-        cp(T.SS[:], PS[PB][:, 0:128], (), ["SS"], [PB])
-        least("HM", 2, PA, 2)
+        least("MN", 0, pa, 0)
+        least("MN", 1, pa, 1)
+        mm(total(pa, 2, (1, 2, 3)), ["IDB", "TL"], [pa])
+        least("HM", 0, pb, 1)
+        least("MN", 2, pb, 0)
+        least("HM", 1, pb, 0)
+        cp(T.SS[:], ps(pb, 0, 128), (), ["SS"], [pb])
+        least("HM", 2, pa, 2)
+        ts(T.INVU[:], T.INVL[:], 0.25 - IOFF, Op.add, r=["INVL"], w=["INVU"])
         mn, hm = T.MN[:, 384:512], T.HM[:, 384:512]
-        hb = (PA, AB[0], AB[1], AB[2])
-        yb = (PB, PA, PB, AB[0])
-        for c in range(4):
-            rs = range(4 * c, 4 * c + 4)
+        hb = (pa, zb[0], zb[1], zb[2])
+        yb = (pb, pa, pb, zb[0])
+
+        def lhs(r):
+            return T.BR[:, 128 * r:128 * r + 128]
+
+        def cl(k, r):
+            return ps(k, 128 * (r % 4), 128 * (r % 4) + 128)
+
+        for kind, c in MEND:
+            c = int(c)
+            rs, part = range(4 * c, 4 * c + 4), slice(512 * c, 512 * c + 512)
             br = [("BR", r) for r in rs]
-
-            def lhs(r):
-                return T.BR[:, 128 * r:128 * r + 128]
-
-            def col(k, r):
-                return PS[k][:, 128 * (r % 4):128 * (r % 4) + 128]
-
-            mm([(col(AB[c], r), lhs(r), mn, False, r % 4 == 3) for r in rs], br + [("MN", 3)], [AB[c]])
-            act(T.CS[:, 512 * c:512 * c + 512], PS[AB[c]][:], Fn.Identity, (), [("CS", c)], [AB[c]], bias=225.0, scale=16.0)
-            mm([(col(hb[c], r), lhs(r), hm, True, True) for r in rs], br + [("HM", 3)], [hb[c]])
-            seq = []
-            for r in rs:
-                seq += [(col(yb[c], r), T.IDB[:], T.AC[:, r::16], True, False), (col(yb[c], r), lhs(r), T.SS[:], False, True)]
-            mm(seq, br + ["SS", "IDB", "AC"], [yb[c]])
-            qq = T.QQ[:, 512 * (c % 2):512 * (c % 2) + 512]
-            tt(qq, PS[hb[c]][:], T.CS[:, 512 * c:512 * c + 512], Op.min, [("CS", c)], [("QQ", c % 2)], [hb[c]])
-            tt(T.R[:, 512 * c:512 * c + 512], PS[yb[c]][:], qq, Op.min, [("QQ", c % 2)], [("R", c)], [yb[c]])
+            if kind == "Z":
+                mm([(cl(zb[c], r), lhs(r), mn, False, r % 4 == 3) for r in rs], br + [("MN", 3)], [zb[c]])
+                act(T.CS[:, part], ps(zb[c]), Fn.Identity, (), [("CS", c)], [zb[c]], bias=225.0, scale=16.0)
+            elif kind == "H":
+                mm([(cl(hb[c], r), lhs(r), hm, True, True) for r in rs], br + [("HM", 3)], [hb[c]])
+            elif kind == "Y":
+                seq = []
+                for r in rs:
+                    seq += [(cl(yb[c], r), T.IDB[:], T.AC[:, r::16], True, False), (cl(yb[c], r), lhs(r), T.SS[:], False, True)]
+                mm(seq, br + ["SS", "IDB"] + ac, [yb[c]])
+            elif kind == "q":
+                tt(T.QQ[:, part], ps(hb[c]), T.CS[:, part], Op.min, [("CS", c)], [("QQ", c)], [hb[c]])
+            else:
+                tt(T.R[:, part], ps(yb[c]), T.QQ[:, part], Op.min, [("QQ", c)], [("R", c)], [yb[c]])
+        strides(1)
         SL = T["SL%d" % rank]
         rr = [("R", c) for c in range(4)] + ["INVU"]
-        act(SL[:, 0:1024], T.R[:].indirect(T.INVU[:, 0:64]), Fn.Relu, rr, [("sl", rank, 0)], bias=15.0)
-        ts(SL[:, 1024:], T.R[:].indirect(T.INVU[:, 64:128]), 15.0, Op.add, 0.0, Op.max, r=rr, w=[("sl", rank, 1)])
-        send(direct, SL[:], SL[:], "sl%d" % rank, [("sl", rank, 0), ("sl", rank, 1)])
-        for q, dd in passes:
-            send([dd], T["SL%d" % q][:], T["SL%d" % q][:], "sl%d" % q, [("sl", q, 0)])
+        act(SL[:, 0:1024], T.R[:].indirect(T.INVU[:, 0:64]), Fn.Relu, rr, [("sl", rank)], bias=15.0)
+        ts(SL[:, 1024:], T.R[:].indirect(T.INVU[:, 64:128]), 15.0, Op.add, 0.0, Op.max, r=rr, w=[("fsl", rank)])
+        for call in calls_of(rank, mended):
+            send(call, "SL")
 
     for t in range(B * NS):
         step(t)

from concourse.bass import DstId, RemoteDMATransfer
from concourse.mybir import AluOpType as Op, ActivationFunctionType as Fn

N, NV, NE, P, S, B = 4, 2048, 1024, 1024, 3, 2
NS = N * S
IOFF = 32
PASS = 2
IOT0 = 96
ALPHA = 123 / 2 ** 14
OH, OR = 24576, 16768
SCATTER = [0, 40] + [4, 0, 0, 0] * 4 + [0] * 5 + [72]
REORDER = [0] * 11 + [16, 0, 0] * 4 + [64]
KPLAN = [0] * 2 + [1] * 21 + [3] + [1] * 24
BY_DMA = [n for n in range(2, 19) if n % 8 not in (3, 6)] + list(range(19, 24)) + [n for n in range(27, 40) if n % 4 in (0, 3)]
JOIN = [22]
NACC = len(JOIN)
RING = 12
KR = 12
SUMS = [0] * 4 + [1] * 17 + [0] * 4 + [1] * 23
FUSED = [21, 22, 23]
MENDL = 20
GA = (128, 256, 128)
LW = 128
ORDER = "mWcPazPVaPLidLLLAAs"
MEND = "Z0 H0 Z1 Y0 q0 Z2 H1 Y1 q1 r0 Z3 H2 Y2 q2 r1 H3 Y3 q3 r2 r3".split()

SCRATCH = {
    "PX": ("sbuf", [128, 128], "int32"), "PY": ("sbuf", [128, 128], "int32"), "VX": ("sbuf", [128, 128], "int32"),
    "VY": ("sbuf", [128, 128], "int32"), "EN": ("sbuf", [128, 128], "int32"), "FM": ("sbuf", [128, 64], "int32"),
    "COR": ("sbuf", [128, 128], "int32"),
    "IOI": ("sbuf", [128, 144], "int32"), "PCI": ("sbuf", [128, 4], "int32"), "PCF": ("sbuf", [128, 16], "float32"),
    "WL": ("sbuf", [128, 144], "bfloat16"), "WY": ("sbuf", [128, 136], "bfloat16"), "GH": ("sbuf", [128, 136], "float16"),
    "GR": ("sbuf", [128, 136], "float16"), "S0": ("sbuf", [128, 136], "float16"), "S1": ("sbuf", [128, 136], "float16"),
    "IDB": ("sbuf", [128, 128], "bfloat16"), "IDF": ("sbuf", [128, 128], "float32"), "IDH": ("sbuf", [128, 128], "float16"),
    "I8": ("sbuf", [128, 128], "bfloat16"), "I254": ("sbuf", [128, 128], "float16"),
    "CK": ("sbuf", [128, 512], "bfloat16"), "ONE": ("sbuf", [128, 512], "bfloat16"),
    "ZB": ("sbuf", [128, 512], "bfloat16"), "BD": ("sbuf", [128, 128], "bfloat16"), "SEL": ("sbuf", [128, 16], "float32"),
    "M2": ("sbuf", [128, 128], "bfloat16"), "BR": ("sbuf", [128, 2048], "bfloat16"),
    "I1": ("sbuf", [128, 128], "int32"), "I2": ("sbuf", [128, 128], "int32"), "I3": ("sbuf", [128, 128], "int32"),
    "F1": ("sbuf", [128, 144], "float32"), "F2": ("sbuf", [128, 128], "float32"), "H1": ("sbuf", [128, 128], "bfloat16"),
    "PH": ("sbuf", [128, 512], "float16"), "X0": ("sbuf", [128, 256], "float32"), "DH": ("sbuf", [128, 256], "float16"),
    "XS": ("sbuf", [128, 192], "float32"), "D0": ("sbuf", [128, 384], "bfloat16"), "D1": ("sbuf", [128, 576], "float32"),
    "SC": ("sbuf", [128, 768], "float16"), "CQ": ("sbuf", [128, 256], "bfloat16"),
    "DR": ("sbuf", [128, 128], "float16"),
    "IL": ("sbuf", [128, 128 * B * NS], "uint16"), "A": ("sbuf", [128, P * B * NS], "bfloat16"),
    "K": ("sbuf", [128, 512 * KR], "bfloat16"), "PR": ("sbuf", [128, 1024], "bfloat16"), "AK": ("sbuf", [128, 2048], "float16"),
    "LD": ("sbuf", [128, 1024 * NACC], "float32"),
    "AD": ("sbuf", [128, 512 * RING], "float32"),
    "CU": ("sbuf", [128, 128], "uint16"), "PU": ("sbuf", [128, 128], "uint16"), "IOT": ("sbuf", [128, 2048], "float32"),
    "INVW": ("sbuf", [128, 2048], "float32"), "INVL": ("sbuf", [128, 128], "float32"), "INVU": ("sbuf", [128, 128], "uint16"),
    "AC": ("sbuf", [128, 2048], "bfloat16"), "CS": ("sbuf", [128, 2048], "bfloat16"), "QQ": ("sbuf", [128, 2048], "bfloat16"),
    "R": ("sbuf", [128, 2048], "bfloat16"),
    "KM": ("sbuf", [128, 512], "bfloat16"), "TY": ("sbuf", [128, 512], "bfloat16"), "TO": ("sbuf", [128, 512], "bfloat16"),
    "TL": ("sbuf", [128, 512], "bfloat16"), "NF": ("sbuf", [128, 64], "float32"),
    "Z2": ("sbuf", [128, 64], "float32"), "SG": ("sbuf", [128, 64], "bfloat16"),
    "MN": ("sbuf", [128, 512], "bfloat16"), "HM": ("sbuf", [128, 512], "bfloat16"), "SS": ("sbuf", [128, 128], "bfloat16"),
    "E0": ("sbuf", [128, 64], "float32"), "E1": ("sbuf", [128, 64], "int32"), "E2": ("sbuf", [128, 64], "int32"),
    "YE": ("sbuf", [128, 128], "float32"), "YL": ("sbuf", [128, 1024], "float32"),
}
for _q in range(N):
    SCRATCH["TAB%d" % _q] = ("sbuf", [128, NV + 2 * NE], "bfloat16")
    SCRATCH["SL%d" % _q] = ("sbuf", [128, NV], "bfloat16")
for _b in range(4):
    SCRATCH["PS%d" % _b] = ("psum", [128, 1024], "float32")
SEMAPHORES = (["cv", "cs", "cp", "cg", "sent", "tm"] + [_p + str(_q) for _q in range(N) for _p in ("slab", "spow", "kap", "sl", "fslab", "fspow", "fkap", "fsl")]
              + ["d%d" % _i for _i in range(14 + len(BY_DMA))])

LB, AB, PB, QB = (0, 1), (2, 3), (5, 6), (4, 7)


def bits(engines):
    m = 0
    for e in engines:
        m |= 1 << e
    return m


def rank_program(g, core, T, topo):
    rank = T.rank_of(core)
    if rank is None:
        return
    cores = T.cores
    eng = {"v": g.vector, "s": g.scalar, "p": g.tensor, "g": g, "y": g.sync}
    count = {}
    known = {q: {} for q in eng}
    wrote, read, bank = {}, {}, {}
    ndma = [0]

    def wait(q, ev):
        sem, val, clock, _ = ev
        if known[q].get(sem, 0) >= val:
            return
        eng[q].wait_ge(T.sem[sem], val)
        for k, x in list(clock.items()) + [(sem, val)]:
            if known[q].get(k, 0) < x:
                known[q][k] = x

    def op(q, fn, r=(), w=(), b=(), dma=False, remote=0):
        need = [wrote[t] for t in r] + [wrote[t] for t in w if t in wrote]
        for t in w:
            need += read.get(t, [])
        for k in b:
            need += [e for qq, e in bank.get(k, {}).items() if qq != q]
        best = {}
        for e in need:
            if q == "p" and e[3] == "p":
                continue
            if e[0] not in best or best[e[0]][1] < e[1]:
                best[e[0]] = e
        for e in sorted(best.values(), key=lambda e: -len(e[2])):
            wait(q, e)
        ins = fn()
        if remote:
            sem, inc = "sent", remote
        elif dma:
            sem, inc = "d%d" % ndma[0], 16
            ndma[0] += 1
            ins.then_inc(T.sem[sem], 16)
        else:
            sem, inc = "c" + q, 1
            ins.then_inc(T.sem[sem], 1)
        count[sem] = count.get(sem, 0) + inc
        ev = (sem, count[sem], dict(known[q]), q)
        if not remote:
            for t in r:
                read.setdefault(t, []).append(ev)
        for t in w:
            wrote[t] = ev
            read[t] = []
        for k in b:
            bank.setdefault(k, {})[q] = ev

    def arrives(token, sem, val):
        count[sem] = val
        wrote[token] = (sem, val, {}, "x")

    def ts(out, in0, s1, o0, s2=None, o1=None, r=(), w=(), b=()):
        if o1 is None:
            op("v", lambda: g.vector.tensor_scalar(out, in0, s1, None, o0), r, w, b)
        else:
            op("v", lambda: g.vector.tensor_scalar(out, in0, s1, s2, o0, o1), r, w, b)

    def tt(out, in0, in1, o, r=(), w=(), b=()):
        op("v", lambda: g.vector.tensor_tensor(out, in0, in1, o), r, w, b)

    def cp(out, in_, r=(), w=(), b=()):
        op("v", lambda: g.vector.tensor_copy(out, in_), r, w, b)

    def fill(out, x, w):
        op("v", lambda: g.vector.memset(out, x), (), w)

    def act(out, in_, f, r=(), w=(), b=(), **kw):
        op("s", lambda: g.scalar.activation(out, in_, f, **kw), r, w, b)

    def mm(seq, r=(), b=()):
        def run():
            ins = None
            for out, lhsT, rhs, start, stop in seq:
                ins = g.tensor.matmul(out, lhsT, rhs, start, stop)
            return ins
        op("p", run, r, (), b)

    def ps(k, c0=0, c1=512):
        return T["PS%d" % (k // 2)][:, 512 * (k % 2) + c0:512 * (k % 2) + c1]

    def near(a, b):
        return cores[b] in topo.cores_of(cores[a])

    def lanes(a):
        far = [d for d in range(N) if not near(a, d)]
        mate = [d for d in range(N) if d != a and near(a, d)]
        off = topo.engines(cores[a], cores[far[0]])
        on = [e for e in topo.engines(cores[a], cores[mate[0]]) if e not in off]
        return off, on

    def source_of(q, d):
        if near(q, d):
            return q
        first = min((x for x in range(N) if near(x, d)), key=lambda x: (q - x) % N)
        return q if first == d else first

    def calls_of(a, parts):
        mate = [d for d in range(N) if d != a and near(a, d)][0]
        far = {q: [d for d in range(N) if not near(q, d) and source_of(q, d) == q][0] for q in (a, mate)}
        off, on = lanes(a)
        out = []
        if (a - far[a]) % N == 1:
            for part, c0, c1 in parts:
                m = (c0 + c1) // 2
                out.append([(far[a], a, part, c0, m, off, part), (mate, a, part, m, c1, on, "f" + part)])
            for part, c0, c1 in parts:
                m = (c0 + c1) // 2
                out.append([(far[mate], mate, part, m, c1, off, part), (mate, a, part, c0, m, on, part)])
        else:
            out += [[(mate, a, part, c0, c1, off + on, part)] for part, c0, c1 in parts]
            out += [[(far[mate], mate, part, (c0 + c1) // 2, c1, off, part)] for part, c0, c1 in parts]
            out += [[(far[a], a, part, c0, (c0 + c1) // 2, off, part)] for part, c0, c1 in parts]
        return out

    def passes_of(a, parts, j):
        mate = [d for d in range(N) if d != a and near(a, d)][0]
        q, (off, on) = (a + j) % N, lanes(a)
        if near(a, q) or source_of(q, mate) != a:
            return []
        return [[(mate, q, part, c0, c1, on if j == 1 else off + on, part)] for part, c0, c1 in parts]

    def expect(parts):
        total = {}
        for a in range(N):
            for call in calls_of(a, parts) + [x for j in range(1, N) for x in passes_of(a, parts, j)]:
                for d, q, part, c0, c1, es, sem in call:
                    if d == rank:
                        total[(sem, q)] = total.get((sem, q), 0) + len(es)
        for (sem, q), n in total.items():
            arrives((sem, q), sem + str(q), n)

    def whole(part, q):
        return [x for x in ((part, q), ("f" + part, q)) if x in wrote]

    def send(call, buf):
        trs, r = [], []
        for d, q, part, c0, c1, es, sem in call:
            rid, pid = topo.addr(cores[d], core)
            side = T[buf + str(q)][:, c0:c1]
            trs.append(RemoteDMATransfer(dst_ids=[DstId(rid=rid, pnc=pid)], dma_engine_mask=bits(es), remote_sem=T.sem[sem + str(q)],
                                         src=side, dst=side))
            r += [("f" + part, q)] if ("f" + part, q) in wrote and q != rank else whole(part, q)
        op("g", lambda: g.remote_dma_fused(trs, local_sem=T.sem.sent), r, (), remote=sum(len(x[5]) for x in call))

    def verdict_lane(a, d):
        off, on = lanes(a)
        far = [x for x in range(N) if not near(a, x)]
        h = len(off) // len(far)
        return on[:h] if near(a, d) else off[far.index(d) * h:(far.index(d) + 1) * h]

    tables = [("slab", 0, NV), ("spow", NV, NV + NE), ("kap", NV + NE, NV + 2 * NE)]
    mended = [("sl", 0, NV)]
    expect(tables)
    expect(mended)
    arrives("TL", "tm", sum(len(verdict_lane(a, rank)) for a in range(N) if a != rank))

    TAB = T["TAB%d" % rank]

    def load(q, out, in_, w):
        op(q, lambda: eng[q].dma_start(out, in_), (), [w], dma=True)

    load("s", T.PX[:], T.px[:], "PX")
    load("y", T.PY[:], T.py[:], "PY")
    load("s", T.EN[:], T.en[:], "EN")
    load("y", T.VX[:], T.vx[:], "VX")
    load("s", T.VY[:], T.vy[:], "VY")
    load("y", TAB[:, 0:NV], T.slab[:], ("slab", rank))
    load("s", T.COR[:], T.cor[:], "COR")
    load("s", TAB[:, NV:NV + NE], T.spow[:], ("spow", rank))
    load("y", TAB[:, NV + NE:], T.kap[:], ("kap", rank))
    load("y", T.FM[:], T.fm[:], "FM")

    def positions(i, c0, c1):
        op("g", lambda: g.iota(T.IOT[:, 16 * c0:16 * c1], [[1, c1 - c0], [128, 16]], IOFF + c0, 0,
                               allow_small_or_imprecise_dtypes=True), (), [("IOT", i)])

    op("g", lambda: g.iota(T.PCI[:], [[0, 4]], 0, 1), (), ["PCI"])
    op("g", lambda: g.iota(T.IOI[:], [[1, 144]], 0, 0), (), ["IOI"])
    positions(0, 0, IOT0)
    for k, call in enumerate(calls_of(rank, tables)):
        send(call, "TAB")
        if k == 1:
            positions(1, IOT0, 128)

    ck = ((128.0, 135.0), (-8.0, 0.0))
    for k in range(2):
        fill(T.CK[0:2, 128 * k:128 * k + 128], ck[k][1], [("CK", k)])
    fill(T.ZB[:], 0.0, ["ZB"])
    for k, x in ((1, 112), (2, 15), (3, 8)):
        ts(T.PCI[:, k:k + 1], T.PCI[:, 0:1], x, Op.bitwise_and, r=["PCI"], w=[("PC", k)])
    fill(T.ONE[:], 1.0, ["ONE"])
    cp(T.PCF[:, 0:4], T.PCI[:], ["PCI"] + [("PC", k) for k in (1, 2, 3)], ["PCF"])
    fill(T.D0[:], 0.0, ["D0"])
    for k in range(2):
        fill(T.CK[0:1, 128 * k:128 * k + 128], ck[k][0], [("CK", k)])

    def const(out, k, n, start):
        return (out, T.CK[0:2, 128 * k:128 * k + 128], T.ONE[0:2, 0:n], start, False)

    pk, pg, pr, pf = [T.PCF[:, k:k + 1] for k in range(4)]
    col = {}

    def column(name, x, y):
        k = 5 + len(col)
        col[name] = T.PCF[:, k:k + 1]
        ts(col[name], pf, (y - x) / 8, Op.mult, x, Op.add, r=["PCF"], w=[name])

    tk = T.PCF[:, 4:5]
    ts(tk, pk, pf, Op.subtract, 8.0, Op.add, r=["PCF"], w=["tk"])
    column("v0", 1.0, 0.0)
    column("v1", 0.0, 1.0)
    column("vh", 1 / 16, 4.0)
    column("vr", -4.0, -128.0)
    column("rs", 1 / 64, 1 / 32)
    column("ro", OR - (OH + 504) / 64, OR - (OH + 248) / 32)
    column("wr", -64.0, -32.0)
    column("cs", 1 / (4 * ALPHA), 0.0)
    ts(T.F1[:], T.IOI[:], pg, Op.subtract, 11.0, Op.subtract, r=["IOI", "PCF"], w=["F1"])
    ts(T.IDF[:], T.IOI[:, 0:128], pk, Op.is_equal, r=["IOI", "PCF"], w=["IDF"])
    ts(T.SEL[:], T.IOI[:, 0:16], pr, Op.is_equal, r=["IOI", "PCF"], w=["SEL"])
    ts(T.I2[:], T.IOI[:, 0:128], 112, Op.bitwise_and, r=["IOI"], w=["I2"])
    act(T.YL[:, 0:144], T.F1[:], Fn.Abs, ["F1"], ["F2"])
    ts(T.S0[:], T.IOI[:, 0:136], tk, Op.is_equal, col["v0"], Op.mult, r=["IOI", "tk", "v0"], w=["S0"])
    ts(T.BD[:], T.I2[:], pg, Op.is_equal, r=["I2", "PCF"], w=["BD"])
    for name, x in (("IDB", 1.0), ("I8", 8.0)):
        act(T[name][:], T.IDF[:], Fn.Copy, ["IDF"], [name], scale=x)
    act(T.QQ[:, 0:128], T.IDF[:], Fn.Copy, ["IDF"], [("QQ", 0)], scale=128.0)
    for k in range(16):
        act(T.BR[:, 128 * k:128 * k + 128], T.BD[:], Fn.Copy, ["BD", "SEL"], [("BR", k)], scale=T.SEL[:, k:k + 1])

    def vl(t, h, c0=0, c1=32):
        o = 128 * t + 32 + 32 * h
        return T.IL[:, o + c0:o + c1]

    def el(t, h):
        o = 128 * t + 96 * h
        return T.IL[:, o:o + 32]

    ts(T.I1[:], T.PY[:], 4, Op.arith_shift_right, r=["PY"], w=["I1"])
    ts(T.I2[:], T.PX[:], 4, Op.arith_shift_right, r=["PX"], w=["I2"])
    ts(T.S1[:], T.IOI[:, 0:136], tk, Op.is_equal, col["v1"], Op.mult, r=["IOI", "tk", "v1"], w=["S1"])
    ts(T.I3[:], T.I1[:], 64.0, Op.mult, r=["I1"], w=["I3"])
    ts(T.WY[:], T.YL[:, 0:136], 4.0, Op.is_equal, -ALPHA, Op.mult, r=["F2"], w=["WY"])
    cp(T.PH[:, 0:128], T.PX[:], ["PX"], [("PH", 0)])
    tt(T.I1[:], T.I3[:], T.I2[:], Op.add, ["I3", "I2"], ["I1"])
    for h in range(2):
        ts(el(0, h), T.EN[:, 32 * h:32 * h + 32], 1 / 64, Op.mult, -31.5 / 64, Op.add, r=["EN"], w=[("EL", 0, h)])
    cp(T.PH[:, 128:256], T.PY[:], ["PY"], [("PH", 1)])
    cp(vl(0, 0, 0, 64), T.I1[:, 0:64], ["I1"], [("VL", 0, 0), ("VL", 0, 1)])
    ts(T.IDH[:], T.IOI[:, 0:128], pk, Op.is_equal, r=["IOI", "PCF"], w=["IDH"])
    ts(T.I254[:], T.IOI[:, 0:128], pk, Op.is_equal, -254.0, Op.mult, r=["IOI", "PCF"], w=["I254"])
    ts(T.D0[:, 2::3], T.ZB[:, 0:128], col["rs"], Op.add, r=["ZB", "rs", "D0"], w=["D02"])
    for h in range(2):
        ts(T.D1[:, 384 * h + 2:384 * h + 192:3], T.ZB[:, 0:64], col["ro"], Op.add, r=["ZB", "ro"], w=[("D12", h)])
        ts(T.CQ[:, 192 * h:192 * h + 64], T.ZB[:, 0:64], col["wr"], Op.add, -float(OR), Op.mult, r=["ZB", "wr"], w=[("CQ", h, 0)])
        fill(T.CQ[:, 64 + 96 * h:96 + 96 * h], -1800 / 64, [("CQ", h, 1)])
    fill(T.CQ[:, 96:160], 132.0 * OR - 65 * OH // 16, [("CQ", 2)])
    ts(T.GH[:], T.IOI[:, 0:136], tk, Op.is_equal, col["vh"], Op.mult, r=["IOI", "tk", "vh"], w=["GH"])
    ts(T.GR[:], T.IOI[:, 0:136], tk, Op.is_equal, col["vr"], Op.mult, r=["IOI", "tk", "vr"], w=["GR"])
    ts(T.DR[:], T.IOI[:, 0:128], pk, Op.is_equal, col["wr"], Op.mult, r=["IOI", "PCF", "wr"], w=["DR"])
    fill(T.XS[:, 64:128], 0.0, ["XC"])

    def regroup(u, z):
        return [(ps(AB[z], 128 * u, 128 * u + 128), (T.S0, T.S1)[u][:, 8 - 8 * f:136 - 8 * f],
                 T.PH[:, 256 * z + 128 * f:256 * z + 128 * f + 128], f == 0, f == 1 and z == 1) for f in range(2)]

    def state():
        cp(T.PH[:, 256:384], T.VX[:], ["VX"], [("PH", 2)])
        cp(T.PH[:, 384:512], T.VY[:], ["VY"], [("PH", 3)])
        mm(regroup(0, 1) + regroup(1, 1), ["S0", "S1", ("PH", 2), ("PH", 3)], [AB[1]])
        ts(T.I2[:], T.COR[:], 15, Op.bitwise_and, r=["COR"], w=["I2"])
        ts(T.I3[:], T.COR[:], 4, Op.arith_shift_right, r=["COR"], w=["I3"])
        ts(T.F2[:], T.I2[:], 128.0, Op.mult, r=["I2"], w=["F3"])
        for u in range(2):
            cp(T.DH[:, u::2], ps(AB[1], 128 * u, 128 * u + 128), w=[("DH", u)], b=[AB[1]])
        for u in range(2):
            mm(regroup(u, 0) + [(ps(AB[0], 128 * u, 128 * u + 128), T.I254[:], T.DH[:, u::2], False, True)],
               ["S0", "S1", "I254", ("PH", 0), ("PH", 1), ("DH", u)], [AB[0]])
        tt(T.I2[:], T.F2[:], T.I3[:], Op.add, ["F3", "I3"], ["I2"])
        begin(0)
        cp(T.PU[:], T.I2[:], ["I2"], ["PU"])
        for u in range(2):
            ts(T.X0[:, u::2], ps(AB[0], 128 * u, 128 * u + 128), OH - 7.5, Op.add, w=[("X0", u)], b=[AB[0]])
        places(0)
        strides(0)

    def uc(h):
        return ps(QB[h], 64, 96) if h == 0 else ps(QB[h], 32, 64)

    def vc(h):
        return ps(QB[h], 96, 128) if h == 0 else ps(QB[h], 0, 32)

    def wc(h):
        return ps(QB[h], 64 * h, 64 * h + 64)

    def yc(h):
        return ps(PB[h], 0, 64)

    def dc(h):
        return ps(PB[h], 64, 128)

    def kept(h):
        return T.D1[:, 288 * h + 1:288 * h + 288:3]

    def begin(b):
        dh = [("DH", u) for u in range(2)]
        ts(T.D1[:, 193:384:3], T.EN[:, 64 * b:64 * b + 64], 1 / 64, Op.mult, r=["EN"], w=[("US", 0), ("US", 1)])
        for h in range(2):
            c = 128 * b + 64 * h
            cp(T.D1[:, 384 * h:384 * h + 192:3], T.DH[:, c:c + 64], dh, [("D10", h)])

    def places(b):
        for h in range(2):
            c = 128 * b + 64 * h
            cp(T.D1[:, 384 * h + 1:384 * h + 192:3], T.X0[:, c:c + 64], [("X0", 0), ("X0", 1)], [("XD", h)])

    def strides(b):
        for h in range(2):
            c = 128 * b + 64 * h
            mm([(dc(h), T.IDH[:], T.DH[:, c:c + 64], True, True)], ["IDH", ("DH", 0), ("DH", 1)], [PB[h]])

    def seed(b, h):
        o = 128 * b + 64 * h
        mm([(ps(QB[h], 0, 128), T.IDB[:], T.CQ[:, 128 * h:128 * h + 128], True, False),
            (ps(QB[h], 32 * h, 32 * h + 96), T.IDF[:], kept(h), False, False), (wc(h), T.I254[:], T.DH[:, o:o + 64], False, False)],
           ["IDB", "IDF", "I254", ("CQ", h, 0), ("CQ", h, 1), ("CQ", 2), ("XD", h), ("US", h)], [QB[h]])

    for k in LB:
        mm([(ps(k), T.ZB[:, 0:128], T.ZB[:], True, False)], ["ZB"], [k])

    spare = [
        lambda: cp(T.CU[:], T.COR[:], ["COR"], ["CU"]),
        lambda: ts(T.I3[:], T.IOI[:, 0:128], 15, Op.bitwise_and, r=["IOI"], w=["I3"]),
        lambda: cp(vl(NS, 0, 0, 64), T.I1[:, 64:128], ["I1"], [("VL", NS, 0), ("VL", NS, 1)]),
        lambda: ts(T.H1[:], T.I3[:], pr, Op.is_equal, 64.0, Op.mult, r=["I3", "PCF"], w=["H1"]),
        lambda: ts(T.NF[:], T.FM[:], -1 / 64, Op.mult, r=["FM"], w=["NF"]),
        lambda: tt(T.M2[:], T.H1[:], T.QQ[:, 0:128], Op.add, ["H1", ("QQ", 0)], ["M2"]),
        lambda: ts(T.WL[:], T.F1[:], 4.0, Op.is_equal, -1 / 64, Op.mult, r=["F1"], w=["WL"]),
    ] + [lambda h=h: ts(el(NS, h), T.EN[:, 64 + 32 * h:96 + 32 * h], 1 / 64, Op.mult, -31.5 / 64, Op.add, r=["EN"],
                        w=[("EL", NS, h)]) for h in range(2)]

    def table(t):
        return (rank + (t % NS) // S) % N

    cut = [sum(GA[:i]) for i in range(len(GA) + 1)]

    def gather(t, h):
        q = table(t)
        win = T["TAB%d" % q][:, 0:NV] if t < NS else T["SL%d" % q][:]
        wtok = whole("slab" if t < NS else "sl", q)
        for u in range(len(GA)):
            o = P * t + 512 * h
            act(T.A[:, o + cut[u]:o + cut[u + 1]], win.indirect(vl(t, h, cut[u] // 16, cut[u + 1] // 16)), Fn.Copy,
                wtok + [("VL", t, h)], [("A", t, h, u)])

    def prod(t, h, u):
        q, o = table(t), 128 * t + 96 * h
        sw = T["TAB%d" % q][:, NV:NV + NE].indirect(T.IL[:, o + cut[u] // 16:o + cut[u + 1] // 16])
        o = P * t + 512 * h
        tt(T.PR[:, 512 * h + cut[u]:512 * h + cut[u + 1]], sw, T.A[:, o + cut[u]:o + cut[u + 1]], Op.mult,
           whole("spow", q) + [("EL", t, h), ("A", t, h, u)], [("PR", h, u)])

    def losses(t, h):
        pr_ = [("PR", h, u) for u in range(len(GA))]
        if t % NS == NS - 1:
            mm([(uc(h), T.WL[:, 15 - r:143 - r], T.PR[:, 512 * h + r:512 * h + 512:16], False, r == 15) for r in range(16)],
               ["WL"] + pr_, [QB[h]])
        else:
            mm([const(yc(h), 0, 64, True)]
               + [(yc(h), T.WY[:, 7 - r:135 - r], T.PR[:, 512 * h + r:512 * h + 512:8], False, r == 7) for r in range(8)],
               ["WY", "ONE", ("CK", 0)] + pr_, [PB[h]])

    done = {"A": 0, "k": 0, "a": 0, "L": 0, "add": 0, "copied": 0}
    NL = 512 // LW

    def coefficients():
        n = done["k"]
        if n >= done["A"] or 2 * n > done["add"] + 2 * KR - 2:
            return
        t, h, q = n // 2, n % 2, table(n // 2)
        if n not in FUSED:
            act(T.K[:, 512 * (n % KR):512 * (n % KR) + 512], T["TAB%d" % q][:, NV + NE:].indirect(el(t, h)), Fn.Copy,
                whole("kap", q) + [("EL", t, h)], [("K", n % KR)])
        done["k"] += 1

    def acopy():
        n, u = done["a"] // 2, done["a"] % 2
        if n >= done["k"] or NL * (n - 1) > done["L"]:
            return
        k = AB[n % 2]
        if n in FUSED or (n in BY_DMA and u == 0):
            pass
        elif u == 0:
            mm([const(ps(k), 1, 512, True)], ["ONE", ("CK", 1)], [k])
        else:
            mm([(ps(k), T.IDB[:], T.A[:, 512 * n:512 * n + 512], n in BY_DMA, True)],
               ["IDB"] + [("A", n // 2, n % 2, x) for x in range(len(GA))], [k])
        done["a"] += 1

    def lmul():
        n, u = done["L"] // NL, done["L"] % NL
        if 2 * n + 2 > done["copied"] or 2 * n > done["add"] + 2:
            if spare:
                spare.pop(0)()
            return
        o = 512 * (n % 4) + LW * u
        out, tok = T.AK[:, o:o + LW], ("AK", n % 4, u)
        if n in BY_DMA:
            x = BY_DMA.index(n) % RING
            while len(pending) >= RING:
                summed()
            out, tok = T.AD[:, 512 * x + LW * u:512 * x + LW * u + LW], ("AD", x, u)
        if n in FUSED:
            t, h, q = n // 2, n % 2, table(n // 2)
            c = 128 * t + 96 * h + LW * u // 16
            tt(out, T["TAB%d" % q][:, NV + NE:].indirect(T.IL[:, c:c + LW // 16]), T.A[:, 512 * n + LW * u:512 * n + LW * u + LW],
               Op.mult, whole("kap", q) + [("EL", t, h)] + [("A", t, h, x) for x in range(len(GA))], [tok])
        else:
            o = 512 * (n % KR) + LW * u
            tt(out, ps(AB[n % 2], LW * u, LW * u + LW), T.K[:, o:o + LW], Op.mult, [("K", n % KR)], [tok], [AB[n % 2]])
        done["L"] += 1

    def ladd():
        n, u = done["add"] // 2, done["add"] % 2
        if NL * (n + u) > done["L"] or n >= done["k"]:
            return
        h, o, last = n % 2, 512 * (n % 4), n // 2 == B * NS - 1 and u == 1
        if n in BY_DMA:
            if u == 1:
                pending.append(n)
        elif u == 0:
            mm([(ps(LB[h]), T.I8[:], T.K[:, 512 * (n % KR):512 * (n % KR) + 512], False, False)], ["I8", ("K", n % KR)], [LB[h]])
        else:
            mm([(ps(LB[h]), T.IDH[:], T.AK[:, o:o + 512], False, last)], ["IDH"] + [("AK", n % 4, x) for x in range(NL)], [LB[h]])
        done["add"] += 1
        if n // 2 in JOIN:
            assert not pending
            x = NACC * h + JOIN.index(n // 2)
            mm([(ps(LB[h], 256 * u, 256 * u + 256), T.IDF[:], T.LD[:, 512 * x + 256 * u:512 * x + 256 * u + 256], False, False)],
               ["IDF", ("LD", x)], [LB[h]])
        if last:
            act(T.YL[:, 512 * h:512 * h + 512], ps(LB[h]), Fn.Exp, (), [("YL", h), "F2"], [LB[h]], scale=-1.0 / 128)
            op("y", lambda: g.sync.dma_start(T.yl[:, 512 * h:512 * h + 512], T.YL[:, 512 * h:512 * h + 512]), [("YL", h)], (), dma=True)

    pending, turn = [], [0, 0]

    def summed():
        if pending:
            n = pending.pop(0)
            x, y = NACC * (n % 2) + turn[n % 2] % NACC, BY_DMA.index(n) % RING
            turn[n % 2] += 1
            kw = {"accum_op": Op.add} if ("LD", x) in wrote else {}
            op("g", lambda: g.dma_start(T.LD[:, 512 * x:512 * x + 512], T.AD[:, 512 * y:512 * y + 512], **kw),
               [("AD", y, z) for z in range(NL)], [("LD", x)], dma=True)

    def lrun(items):
        end = max(min(done["add"] // 2 + items, done["A"]), (done["a"] + 1) // 2)
        while done["add"] < 2 * end:
            coefficients()
            done["copied"] = done["a"]
            for _ in range(2):
                if done["a"] < 2 * end:
                    acopy()
            for _ in range(2):
                for _ in range(NL // 2):
                    lmul()
                ladd()

    def after(t, h):
        ph = 2 * t + h
        done["A"] = ph + 1
        for _ in range(KPLAN[ph]):
            coefficients()
        if t < NS and REORDER[ph]:
            c0 = sum(REORDER[:ph])
            c1 = c0 + REORDER[ph]
            act(T.AC[:, 16 * c0:16 * c1], TAB[:, 0:NV].indirect(T.CU[:, c0:c1]), Fn.Identity,
                [("slab", rank), "CU"], [("AC", ph)], bias=-15.0)
        if t < NS and SCATTER[ph]:
            c0 = sum(SCATTER[:ph])
            c1 = c0 + SCATTER[ph]
            act(T.INVW[:].indirect(T.PU[:, c0:c1]), T.IOT[:, 16 * c0:16 * c1], Fn.Silu,
                ["PU", ("IOT", 0)] + ([("IOT", 1)] if c1 > IOT0 else []), ["INVW"])
            if c1 == 128:
                op("y", lambda: g.sync.dma_start(T.INVL[:], T.INVW[0::16, :]), ["INVW"], ["INVL"], dma=True)

    def phase(t, h, other):
        b, i = t // NS, t % NS
        c = slice(64 * h, 64 * h + 64)
        c32 = slice(32 * h, 32 * h + 32)
        mcol = T.D0[:, 192 * h + 1:192 * h + 192:3]
        if other and (i, h) != (0, 0):
            gather(*other)
            after(*other)
        nbig = [0]
        done["copied"] = done["a"]
        if (2 * i + h + PASS) % (2 * S) == 0:
            for call in passes_of(rank, (tables, mended)[b], (2 * i + h + PASS) // (2 * S)):
                send(call, ("TAB", "SL")[b])
        for _ in range(SUMS[2 * t + h]):
            summed()

        def products():
            if other and nbig[0] < len(GA):
                prod(other[0], other[1], nbig[0])
                nbig[0] += 1
                if nbig[0] == len(GA):
                    losses(*other)

        def save():
            tt(kept(h), ps(QB[h], 32 * h, 32 * h + 96), T.XS[:, 96 * h:96 * h + 96], Op.add,
               [("XS", h), "XC"], [("XD", h), ("US", h)], [QB[h]])
            if i == NS - 2:
                seq = [(uc(h), T.IDF[:], T.D1[:, 193 + 96 * h:288 + 96 * h:3], True, False)]
                if b == 0:
                    seq += [(uc(h), T.IDF[:], T.NF[:, c32], False, False)]
                mm(seq, ["IDF", "NF", ("US", h)], [QB[h]])

        def scan():
            op("v", lambda: g.vector.tensor_tensor_scan(T.SC[:, 192 * h + 192:192 * h + 384], T.D0[:, 192 * h:192 * h + 192],
                                                        T.D1[:, 384 * h:384 * h + 192], 0.0, Op.mult, Op.add),
               [("MM", h), "D02", ("D10", h), ("XD", h), ("D12", h)], [("SC", h)])

        def voxels():
            o, uv = 192 * h + 192, ps(QB[h], 64 - 64 * h, 128 - 64 * h)
            seq = [(wc(h), T.DR[:], T.SC[:, o + 2:o + 192:3], False, False)]
            seq += [(uv, T.GH[:, 8 - 8 * u:136 - 8 * u], T.SC[:, 384 * h + 1 + 3 * u:384 * h + 384:6], False, False) for u in range(2)]
            seq += [(vc(h), T.GR[:, 8 - 8 * u:136 - 8 * u], T.SC[:, o + 2 + 3 * u:o + 192:6], False, u == 1) for u in range(2)]
            mm(seq, ["GH", "GR", "DR", ("SC", h), ("CC", h)], [QB[h]])

        def lists():
            o = 128 * (t + 1) + 64 * h
            ts(T.IL[:, o:o + 64], ps(QB[h], 64 - 64 * h, 128 - 64 * h), -31.5 / 64, Op.add,
               w=[("VL", t + 1, h), ("EL", t + 1, h)], b=[QB[h]])

        if t == B * NS - 1:
            if h == 0:
                lrun(2 * B * NS - 1 - done["add"] // 2)
                acopy()
                acopy()
            for _ in GA:
                products()
            lrun(1)
            ts(T.E1[:, c32], uc(h), 64.0, Op.mult, 0.0, Op.max, w=[("E1", h)], b=[QB[h]])
        elif i == NS - 1:
            tt(T.Z2[:, c32], uc(h), T.NF[:, c32], Op.max, ["NF"], [("Z2", h)], [QB[h]])
            products()
            ts(T.SG[:, c32], T.Z2[:, c32], -1 / 64, Op.max, 1 / 64, Op.min, r=[("Z2", h)], w=[("SG", h)])
            for _ in GA:
                products()
        else:
            calls = {
                "m": lambda: ts(mcol, yc(h), 255.0, Op.max, 258.0, Op.min, r=["D0"], w=[("MM", h)], b=[PB[h]]),
                "c": lambda: ts(T.SC[:, 576 * h + 1:576 * h + 192:3], yc(h), 263 - 1800 * ALPHA, Op.subtract, col["cs"], Op.mult,
                                r=["cs"], w=[("CC", h)], b=[PB[h]]),
                "d": lambda: tt(T.XS[:, 128 * h:128 * h + 64], dc(h), mcol, Op.mult, [("MM", h)], [("XS", h)], [PB[h]]),
                "z": scan, "W": lambda: seed(b, h), "s": save, "V": voxels, "i": lists, "P": products, "a": acopy, "L": lmul, "A": ladd,
            }
            for x in ORDER:
                calls[x]()
            if b == 0 and i % S == S - 2 and h == 1:
                j = 128 * (i // S)
                vv = [("VL", t + 1, 0), ("VL", t + 1, 1)]
                ts(T.KM[:, j:j + 64], vl(t + 1, 0, 0, 64), float(P), Op.is_lt, r=vv, w=[("KM", i // S, 0)])
                ts(T.KM[:, j + 64:j + 128], vl(t + 1, 0, 0, 64), float(P), Op.is_ge, r=vv, w=[("KM", i // S, 1)])

    def energies(b):
        ts(T.E2[:], T.E1[:], 1023, Op.bitwise_and, r=[("E1", 0), ("E1", 1)], w=["E2"])
        cp(T.YE[:, 64 * b:64 * b + 64], T.E2[:], ["E2"], [("YE", b)])

    def step(t):
        if t % NS == 0:
            gather(t, 0)
            gather(t, 1)
            if t == 0:
                state()
            after(t, 0)
            after(t, 1)
            for u in range(len(GA)):
                prod(t, 0, u)
            losses(t, 0)
            for _ in range(4):
                acopy()
        while t == S and spare:
            spare.pop(0)()
        phase(t, 0, (t, 1))
        if t == NS - 1:
            phase(t, 1, None)
            mend(t)
        elif t == B * NS - 1:
            phase(t, 1, None)
            energies(1)
            op("y", lambda: g.sync.dma_start(T.ye[:], T.YE[:]), [("YE", 0), ("YE", 1)], (), dma=True)
        else:
            phase(t, 1, (t + 1, 0))

    def band(j):
        return [("KM", j, x) for x in range(2)]

    def mend(t):
        pa, pb = PB
        mm([(ps(pb, 64 * h, 64 * h + 64), T.M2[:], T.SG[:], True, True) for h in range(2)], ["M2", ("SG", 0), ("SG", 1)], [pb])
        for j in (1, 2, 3):
            tt(T.TY[:, 128 * j:128 * j + 128], ps(pb, 0, 128), T.KM[:, 128 * j:128 * j + 128], Op.mult, band(j), [("TY", j)], [pb])
        ts(T.TO[:, 128:512], T.TY[:, 128:512], -1.0, Op.max, 1.0, Op.min, r=[("TY", j) for j in (1, 2, 3)], w=["TO"])
        trs, tot = [], 0
        for j in range(1, N):
            dd = (rank + j) % N
            rid, pid = topo.addr(cores[dd], core)
            trs.append(RemoteDMATransfer(dst_ids=[DstId(rid=rid, pnc=pid)], dma_engine_mask=bits(verdict_lane(rank, dd)),
                                         remote_sem=T.sem.tm, src=T.TO[:, 128 * j:128 * j + 128], dst=T.TL[:, 128 * j:128 * j + 128]))
            tot += len(verdict_lane(rank, dd))
        op("g", lambda: g.remote_dma_fused(trs, local_sem=T.sem.sent), ["TO"], (), remote=tot)
        tt(T.TY[:, 0:128], ps(pb, 0, 128), T.KM[:, 0:128], Op.mult, band(0), [("TY", 0)], [pb])
        tt(T.E0[:], T.Z2[:], T.NF[:], Op.subtract, [("Z2", 0), ("Z2", 1), "NF"], ["E0"])
        ts(T.TO[:, 0:128], T.TY[:, 0:128], -1.0, Op.max, 1.0, Op.min, r=[("TY", 0)], w=["T0"])
        ts(T.E1[:], T.E0[:], 64.0, Op.mult, r=["E0"], w=[("E1", 0), ("E1", 1)])
        ts(T.MN[:, 0:128], T.TO[:, 0:128], 0.0, Op.min, r=["T0"], w=[("MN", 0)])
        begin(1)
        energies(0)
        places(1)
        ac = [("AC", ph) for ph in range(2 * NS) if REORDER[ph]]
        zb = (QB[0], QB[1], AB[0], AB[1])
        for c in range(4):
            if c == 2:
                lrun(MENDL)
            mm([(ps(zb[c]), T.ZB[:, 0:128], T.ZB[:], True, False)]
               + [(ps(zb[c], 128 * k, 128 * k + 128), T.IDB[:], T.AC[:, 4 * c + k::16], False, False) for k in range(4)],
               ["ZB", "IDB"] + ac, [zb[c]])
        tj = [T.TO[:, 0:128]] + [T.TL[:, 128 * j:128 * j + 128] for j in range(1, N)]

        def total(k, cl, js):
            return [(ps(k, 128 * cl, 128 * cl + 128), T.IDB[:], tj[j], n == 0, n == len(js) - 1) for n, j in enumerate(js)]

        def least(name, n, k, cl):
            tt(T[name][:, 128 * n + 128:128 * n + 256], ps(k, 128 * cl, 128 * cl + 128), T[name][:, 128 * n:128 * n + 128],
               Op.min, [(name, n)], [(name, n + 1)], [k])

        mm(total(pa, 0, (0, 1)) + total(pa, 1, (0, 1, 2)), ["IDB", "T0", "TL"], [pa])
        mm(total(pb, 0, (0, 1, 2, 3)) + total(pb, 1, (2, 3)), ["IDB", "T0", "TL"], [pb])
        ts(T.HM[:, 0:128], tj[3], 0.0, Op.min, r=["TL"], w=[("HM", 0)])
        least("MN", 0, pa, 0)
        least("MN", 1, pa, 1)
        mm(total(pa, 2, (1, 2, 3)), ["IDB", "TL"], [pa])
        least("HM", 0, pb, 1)
        least("MN", 2, pb, 0)
        least("HM", 1, pb, 0)
        cp(T.SS[:], ps(pb, 0, 128), (), ["SS"], [pb])
        least("HM", 2, pa, 2)
        ts(T.INVU[:], T.INVL[:], 0.25 - IOFF, Op.add, r=["INVL"], w=["INVU"])
        mn, hm = T.MN[:, 384:512], T.HM[:, 384:512]
        hb = (pa, zb[0], zb[1], zb[2])
        yb = (pb, pa, pb, zb[0])

        def lhs(r):
            return T.BR[:, 128 * r:128 * r + 128]

        def cl(k, r):
            return ps(k, 128 * (r % 4), 128 * (r % 4) + 128)

        for kind, c in MEND:
            c = int(c)
            rs, part = range(4 * c, 4 * c + 4), slice(512 * c, 512 * c + 512)
            br = [("BR", r) for r in rs]
            if kind == "Z":
                mm([(cl(zb[c], r), lhs(r), mn, False, r % 4 == 3) for r in rs], br + [("MN", 3)], [zb[c]])
                act(T.CS[:, part], ps(zb[c]), Fn.Identity, (), [("CS", c)], [zb[c]], bias=225.0, scale=16.0)
            elif kind == "H":
                mm([(cl(hb[c], r), lhs(r), hm, True, True) for r in rs], br + [("HM", 3)], [hb[c]])
            elif kind == "Y":
                seq = []
                for r in rs:
                    seq += [(cl(yb[c], r), T.IDB[:], T.AC[:, r::16], True, False), (cl(yb[c], r), lhs(r), T.SS[:], False, True)]
                mm(seq, br + ["SS", "IDB"] + ac, [yb[c]])
            elif kind == "q":
                tt(T.QQ[:, part], ps(hb[c]), T.CS[:, part], Op.min, [("CS", c)], [("QQ", c)], [hb[c]])
            else:
                tt(T.R[:, part], ps(yb[c]), T.QQ[:, part], Op.min, [("QQ", c)], [("R", c)], [yb[c]])
        strides(1)
        SL = T["SL%d" % rank]
        rr = [("R", c) for c in range(4)] + ["INVU"]
        act(SL[:, 0:1024], T.R[:].indirect(T.INVU[:, 0:64]), Fn.Relu, rr, [("sl", rank)], bias=15.0)
        ts(SL[:, 1024:], T.R[:].indirect(T.INVU[:, 64:128]), 15.0, Op.add, 0.0, Op.max, r=rr, w=[("fsl", rank)])
        for call in calls_of(rank, mended):
            send(call, "SL")

    for t in range(B * NS):
        step(t)
    for sem in sorted(count):
        wait("g", (sem, count[sem], {}, "x"))
